import numpy as np
import ml_dtypes


def mxq(x, axis, fmt="e4m3"):
    dtype, down = {"e4m3": (ml_dtypes.float8_e4m3fn, 7), "e5m2": (ml_dtypes.float8_e5m2, 14)}[fmt]
    v = np.moveaxis(np.asarray(x, np.float32).astype(ml_dtypes.bfloat16).astype(np.float64), axis, -1)
    blocks = v.reshape(v.shape[:-1] + (-1, 32))
    amax = np.abs(blocks).max(-1, keepdims=True)
    byte = np.maximum(np.where(amax > 0, np.frexp(amax)[1] - 1 + 127, 0) - down, 1)
    scale = np.exp2(byte - 127.0)
    codes = (blocks / scale).astype(np.float32).astype(dtype).astype(np.float64)
    return np.moveaxis((codes * scale).reshape(v.shape), -1, axis)


WIDE = False


def mx_kscale(k):
    if not WIDE:
        return np.ones(k)
    levels = np.array([10, -10, 5, -5, 0])
    if k % 512:
        return np.exp2(np.random.permutation(np.resize(levels, k // 32))).repeat(32)
    a = np.empty((k // 512, 16))
    for p in range(k // 512):
        a[p, :8] = np.random.permutation(np.resize(levels, 8))
        for g in range(8):
            far = levels[np.abs(levels - a[p, g]) >= 10]
            a[p, g + 8] = far[np.random.randint(len(far))]
    return np.exp2(a.ravel()).repeat(32)


def f64(x):
    return np.asarray(x).astype(np.float64)


def striped(idx):
    return np.tile(idx.reshape(-1, 16).T, (8, 1)).astype(np.uint16)


def unstriped(offs):
    return offs[:16].T.reshape(-1).astype(np.int64)


E2M1 = np.array([0.0, 0.5, 1.0, 1.5, 2.0, 3.0, 4.0, 6.0, -0.0, -0.5, -1.0, -1.5, -2.0, -3.0, -4.0, -6.0])


def pack_weight(w, fmt):
    k, n = w.shape
    w = f64(np.asarray(w, np.float32).astype(ml_dtypes.bfloat16)).reshape(k // 32, 32, n)
    amax = np.abs(w).max(1)
    if fmt == "e4m3":
        byte = np.frexp(amax)[1] - 1 + 127 - 7
    else:
        mant, ex = np.frexp(amax / 6.0)
        byte = np.where(mant > 0.5, ex, ex - 1) + 127
    byte = np.clip(np.where(amax > 0, byte, 1), 1, 254)
    scaled = (w * np.exp2(127.0 - byte)[:, None, :]).reshape(k, n).astype(np.float32)
    by_word = np.ascontiguousarray(scaled.reshape(k // 512, 128, 4, n).transpose(0, 1, 3, 2))
    if fmt == "e4m3":
        words = by_word.astype(ml_dtypes.float8_e4m3fn).view(np.uint8)
    else:
        c = by_word.astype(ml_dtypes.float4_e2m1fn).view(np.uint8) & 0xF
        words = (c[..., 0::2] | (c[..., 1::2] << 4)).reshape(k // 512, 128, 2 * n)
    return np.ascontiguousarray(words), np.ascontiguousarray(byte.astype(np.uint8).reshape(k // 512, 16, n))


def unpack_weight(words, scales, fmt):
    g, _, n = scales.shape
    words = np.ascontiguousarray(words).reshape(g, 128, n, -1)
    if fmt == "e4m3":
        vals = words.view(ml_dtypes.float8_e4m3fn).astype(np.float64)
    else:
        nib = np.empty((g, 128, n, 4), np.uint8)
        nib[..., 0::2] = words & 0xF
        nib[..., 1::2] = words >> 4
        vals = E2M1[nib]
    vals = vals * np.repeat(np.exp2(scales.astype(np.float64) - 127.0), 8, axis=1)[..., None]
    return vals.transpose(0, 1, 3, 2).reshape(g * 512, n)


def gelu(v):
    return 0.5 * v * (1.0 + np.tanh(np.sqrt(2.0 / np.pi) * (v + 0.044715 * v**3)))


def bf(x):
    return np.asarray(x, np.float32).astype(ml_dtypes.bfloat16)


def planes(Y):
    n, m = Y.shape
    b = f64(bf(Y)).reshape(n // 32, 32, m)
    amax = np.abs(b).max(1)
    byte = np.clip(np.where(amax > 0, np.frexp(amax)[1] - 1 + 127 - 7, 1), 1, 254)
    codes = (b * np.exp2(127.0 - byte)[:, None, :]).reshape(n, m).astype(np.float32).astype(ml_dtypes.float8_e4m3fn).view(np.uint8)
    words = codes.reshape(n // 512, 128, 4, m).transpose(0, 1, 3, 2)
    return np.ascontiguousarray(words), np.ascontiguousarray(byte.astype(np.uint8).reshape(n // 512, 16, m))


K, T, S, H, P, N = 1024, 4096, 1024, 1024, 512, 512


def setup_inputs():
    n = np.random.standard_normal
    s = mx_kscale(K)[:, None]
    u = mx_kscale(H)[:, None]
    d = {}
    d["tab_words"], d["tab_scales"] = pack_weight(n((K, T)) * s, "e2m1")
    d["offs"] = striped(np.random.permutation(T)[:S])
    d["pos1"] = striped(np.random.permutation(S)[:P])
    d["pos2"] = striped(np.random.permutation(S)[:P])
    d["w1"] = (n((K, H)) / K**0.5 / s * u.T).astype(np.float32)
    d["w2_words"], d["w2_scales"] = pack_weight(1.4 * n((K, H)) / K**0.5 / s, "e4m3")
    d["bc"] = (0.8 * n(H)).astype(np.float32)
    d["cgain"] = (1.4 * np.exp(0.3 * n(H)) * u[:, 0]).astype(np.float32)
    d["w3_words"], d["w3_scales"] = pack_weight(n((H, N)) / H**0.5 / u, "e2m1")
    d["ogain"] = np.exp(0.8 * n(N)).astype(np.float32)
    return d


def reference(tab_words, tab_scales, offs, pos1, pos2, w1, w2_words, w2_scales, bc, cgain, w3_words, w3_scales, ogain):
    v = unpack_weight(tab_words, tab_scales, "e2m1")[:, unstriped(offs)]
    w2 = unpack_weight(w2_words, w2_scales, "e4m3")
    w3 = unpack_weight(w3_words, w3_scales, "e2m1")
    att = mxq(f64(w1), 0, "e4m3").T @ v
    raw = (w2.T @ v) + f64(bc)[:, None]
    ctr = f64(cgain)[:, None] * np.tanh(raw)
    first = att[:, unstriped(pos1)] + ctr[:, unstriped(pos2)]
    second = att[:, unstriped(pos2)] + ctr[:, unstriped(pos1)]
    z = np.maximum(first, second)
    y = f64(ogain)[:, None] * (w3.T @ mxq(z, 0, "e4m3"))
    words, scales = planes(y)
    return y, words, scales

@@ -1,0 +1,298 @@
+from contextlib import ExitStack
+
+import concourse.mybir as mybir
+
+K, T, S, H, PAIRS, N = 1024, 4096, 1024, 1024, 512, 512
+FLOPS = 2 * (2 * K * H * S + H * N * PAIRS)
+
+F32 = mybir.dt.float32
+BF16 = mybir.dt.bfloat16
+I32 = mybir.dt.int32
+U32 = mybir.dt.uint32
+U16 = mybir.dt.uint16
+U8 = mybir.dt.uint8
+FP8X4 = mybir.dt.float8_e4m3fn_x4
+FP4X4 = mybir.dt.float4_e2m1fn_x4
+ACT = mybir.ActivationFunctionType
+ALU = mybir.AluOpType
+
+P = 128
+
+
+def tile_list_bout_corner_planner_kernel(
+    tc, tab_words, tab_scales, offs, pos1, pos2, w1, w2_words, w2_scales, bc, cgain,
+    w3_words, w3_scales, ogain, out_0, out_1, out_2,
+):
+    nc = tc.nc
+    with ExitStack() as ctx:
+        keep = ctx.enter_context(tc.tile_pool(name="keep", bufs=1))
+        ring = ctx.enter_context(tc.tile_pool(name="ring", bufs=2))
+        ps1 = ctx.enter_context(tc.psum_pool(name="ps1", bufs=6))
+        ps2 = ctx.enter_context(tc.psum_pool(name="ps2", bufs=2))
+
+        def held(name, shape, dtype, tag=None):
+            return keep.tile(shape, dtype, name=name, tag=tag or name, align_bytes=64)
+
+        offs_t = held("offs_t", [P, S // 16], U16)
+        pos1_t = held("pos1_t", [P, PAIRS // 16], U16)
+        pos2_t = held("pos2_t", [P, PAIRS // 16], U16)
+        tabw = [held("tabw0", [P, T], U16, "stage1"), held("tabw1", [P, T], U16)]
+        tabs = held("tabs", [P, T], U8, "stage0")
+        vw = [held("vw%d" % a, [P, S], U16) for a in range(2)]
+        vs_packed = held("vs_packed", [P, S], U8, "stage2")
+        vs = [held("vs%d" % a, [P, S], U8) for a in range(2)]
+        w2raw = {0: held("w2raw0", [P, 2, 512], I32)}
+        w2c = [held("w2c%d" % b, [P, 2, 512], I32) for b in range(2)]
+        w2s_raw = held("w2s_raw", [P, 2 * H], U8, "stage3")
+        w2s = held("w2s", [P, 4, 512], U8)
+        w3c = held("w3c", [P, 2 * N], U16)
+        w3s_raw = held("w3s_raw", [P, 2 * N], U8)
+        w3s = held("w3s", [P, 2 * N], U8)
+        w1raw = {}
+        w1c = [[held("w1c%d%d" % (b, a), [P, 512], U32) for a in range(2)] for b in range(2)]
+        w1s = [[held("w1s%d%d" % (b, a), [P, 512], U8) for a in range(2)] for b in range(2)]
+        bc_t = held("bc_t", [P, 2, 4], F32)
+        cg_t = held("cg_t", [P, 2, 4], F32)
+        og_t = held("og_t", [P, 4], F32)
+        warm = held("warm", [P, 8], F32)
+        warm_out = held("warm_out", [P, 8], F32)
+
+        nc.vector.memset(w2s_raw[:].bitcast(I32), 0)
+        for q in range(4):
+            (nc.vector if q < 3 else nc.gpsimd).memset(tabs[32 * q : 32 * q + 24, :].bitcast(I32), 0)
+        nc.vector.memset(warm[:], 0.0)
+        for a in range(2):
+            nc.vector.memset(vs[a][:].bitcast(I32), 0)
+
+        nc.sync.dma_start(offs_t[:], offs)
+        for q in range(4):
+            nc.sync.dma_start(
+                tabs[32 * q + 24 : 32 * q + 32, :].bitcast(I32),
+                tab_scales[:, 4 * q : 4 * q + 4, :].bitcast(I32),
+            )
+        w2v = w2_words.rearrange("a p c i -> p a (c i)").bitcast(I32)
+        w1v = w1.rearrange("(a p j) c -> a p j c", a=2, j=4)
+        nc.sync.dma_start(tabw[0][:].bitcast(I32), tab_words[0].bitcast(I32))
+        nc.sync.dma_start(pos1_t[:], pos1)
+        nc.sync.dma_start(pos2_t[:], pos2)
+        nc.sync.dma_start(tabw[1][:].bitcast(I32), tab_words[1].bitcast(I32))
+
+        def load_w1(b, a, tag):
+            w1raw[b, a] = held("w1raw%d%d" % (b, a), [P, 4, 512], F32, tag)
+            nc.sync.dma_start(w1raw[b, a][:], w1v[a, :, :, 512 * b : 512 * b + 512])
+
+        load_w1(0, 0, "stage4")
+        nc.sync.dma_start(w2raw[0][:], w2v[:, :, 0:512])
+        for q in range(4):
+            nc.scalar.dma_start(
+                w2s_raw[32 * q : 32 * q + 4, :].bitcast(I32).rearrange("p (a c) -> p a c", a=2),
+                w2_scales[:, 4 * q : 4 * q + 4, :].rearrange("a r c -> r a c").bitcast(I32),
+            )
+        nc.scalar.activation(warm_out[:], warm[:], ACT.Tanh)
+        nc.gpsimd.dma_start(bc_t[:], bc.rearrange("(b p t) -> p b t", b=2, t=4))
+        nc.gpsimd.dma_start(cg_t[:], cgain.rearrange("(b p t) -> p b t", b=2, t=4))
+        nc.gpsimd.memset(w3s_raw[:].bitcast(I32), 0)
+        for q in range(4):
+            nc.gpsimd.dma_start(
+                w3s_raw[32 * q : 32 * q + 4, :].bitcast(I32).rearrange("p (a c) -> p a c", a=2),
+                w3_scales[:, 4 * q : 4 * q + 4, :].rearrange("a r c -> r a c").bitcast(I32),
+            )
+        nc.gpsimd.dma_start(og_t[:], ogain.rearrange("(p t) -> p t", t=4))
+
+        nc.vector.tensor_copy(vs_packed[:], tabs[:].indirect(offs_t[:]))
+        for a in range(2):
+            first_row = 24 + 4 * a
+            nc.scalar.dma_start(
+                vs[a][0 : P - first_row, :].bitcast(I32), vs_packed[first_row:P, :].bitcast(I32)
+            )
+
+        load_w1(0, 1, "stage0")
+        nc.vector.tensor_copy(vw[0][:], tabw[0][:].indirect(offs_t[:]))
+        w2raw[1] = held("w2raw1", [P, 2, 512], I32, "stage1")
+        nc.sync.dma_start(w2raw[1][:], w2v[:, :, 512:1024])
+        nc.vector.tensor_copy(
+            w2s[:].rearrange("p g (t c i) -> p g c t i", t=4, i=16),
+            w2s_raw[:].rearrange("p (g c i t) -> p g c t i", g=4, t=4, i=16),
+        )
+        w3raw = held("w3raw", [P, 2 * N], U16, "stage2")
+        nc.sync.dma_start(
+            w3raw[:].bitcast(I32).rearrange("p (a c) -> p a c", a=2),
+            w3_words.rearrange("a p c -> p a c").bitcast(I32),
+        )
+
+        def deal_w2(b):
+            nc.vector.tensor_copy(
+                w2c[b][:].rearrange("p a (t c i) -> p a c t i", t=4, i=4),
+                w2raw[b][:].rearrange("p a (c i t) -> p a c t i", t=4, i=4),
+            )
+
+        deal_w2(0)
+        for h in range(2):
+            nc.vector.tensor_copy(
+                vw[1][:, 512 * h : 512 * h + 512], tabw[1][:].indirect(offs_t[:, 32 * h : 32 * h + 32])
+            )
+
+        def round_w1(b, a, on_vector):
+            grouped = held("w1bf%d%d" % (b, a), [P, 4, 128, 4], BF16, "stage3" if a == 1 else "w1bf")
+            dst = grouped[:].rearrange("p t m j -> p m t j")
+            src = w1raw[b, a][:].rearrange("p j (m t) -> p m t j", t=4)
+            if on_vector:
+                nc.vector.tensor_copy(dst, src)
+            else:
+                nc.scalar.copy(dst, src)
+            nc.vector.quantize_mx(
+                out=w1c[b][a][:].bitcast(FP8X4),
+                scales=w1s[b][a][:],
+                in_=grouped[:].rearrange("p t m j -> p (t m j)"),
+            )
+
+        def product(codes, scales, h):
+            acc = ps1.tile([P, 512], F32, name="acc")
+            cols = slice(512 * h, 512 * h + 512)
+            for a in range(2):
+                nc.tensor.matmul_mx(
+                    out=acc[:],
+                    lhsT=codes(a).bitcast(FP8X4),
+                    lhsT_scale=scales(a),
+                    rhs=vw[a][:, cols].bitcast(FP4X4),
+                    rhs_scale=vs[a][:, cols],
+                    start=(a == 0),
+                    stop=(a == 1),
+                )
+            return acc
+
+        ctr = {}
+        att = {}
+        c1 = {}
+        c2 = {}
+
+        def make_ctr(s):
+            b, t = divmod(s, 4)
+            ctr[s] = ring.tile([P, S], F32, name="ctr", bufs=4)
+            for h in range(2):
+                acc = product(
+                    lambda a: w2c[b][:, a, 128 * t : 128 * t + 128],
+                    lambda a: w2s[:, 2 * a + b, 128 * t : 128 * t + 128],
+                    h,
+                )
+                th = ring.tile([P, 512], F32, name="th", bufs=3)
+                nc.scalar.activation(th[:], acc[:], ACT.Tanh, bias=bc_t[:, b, t : t + 1])
+                nc.scalar.activation(
+                    ctr[s][:, 512 * h : 512 * h + 512], th[:], ACT.Copy, scale=cg_t[:, b, t : t + 1]
+                )
+            c1[s] = ring.tile([P, PAIRS], F32, name="c1", bufs=6)
+            c2[s] = ring.tile([P, PAIRS], F32, name="c2", bufs=6)
+            nc.vector.tensor_copy(c2[s][:], ctr[s][:].indirect(pos2_t[:]))
+            nc.vector.tensor_copy(c1[s][:], ctr[s][:].indirect(pos1_t[:]))
+
+        zb = [held("zb%d" % b, [P, 4, PAIRS], BF16) for b in range(2)]
+        zi = [held("zi%d" % b, [P, PAIRS, 4], BF16) for b in range(2)]
+        zc = [held("zc%d" % b, [P, PAIRS], U32) for b in range(2)]
+        zs = [held("zs%d" % b, [P, PAIRS], U8) for b in range(2)]
+
+        def make_att(s):
+            b, t = divmod(s, 4)
+            att[s] = ring.tile([P, S], F32, name="att", bufs=4)
+            for h in range(2):
+                acc = product(
+                    lambda a: w1c[b][a][:, 128 * t : 128 * t + 128],
+                    lambda a: w1s[b][a][:, 128 * t : 128 * t + 128],
+                    h,
+                )
+                nc.scalar.copy(att[s][:, 512 * h : 512 * h + 512], acc[:])
+
+        def make_z(s, lo, hi):
+            b, t = divmod(s, 4)
+            first = ring.tile([P, hi - lo], F32, name="first")
+            second = ring.tile([P, hi - lo], F32, name="second")
+            o = slice(lo // 16, hi // 16)
+            nc.vector.tensor_tensor(first[:], att[s][:].indirect(pos1_t[:, o]), c2[s][:, lo:hi], ALU.add)
+            nc.vector.tensor_tensor(second[:], att[s][:].indirect(pos2_t[:, o]), c1[s][:, lo:hi], ALU.add)
+            nc.vector.tensor_tensor(zb[b][:, t, lo:hi], first[:], second[:], ALU.max)
+
+        def quantize_z(b, lo, hi, on_vector):
+            dst = zi[b][:, lo:hi, :].rearrange("p (c i) t -> p c t i", i=4)
+            src = zb[b][:, :, lo:hi].rearrange("p t (c i) -> p c t i", i=4)
+            if on_vector:
+                nc.vector.tensor_copy(dst, src)
+            else:
+                nc.scalar.copy(dst, src)
+            nc.vector.quantize_mx(
+                out=zc[b][:, lo:hi].bitcast(FP8X4),
+                scales=zs[b][:, lo:hi],
+                in_=zi[b][:, lo:hi, :].rearrange("p m t -> p (m t)"),
+            )
+
+        y = [held("y%d" % h, [P, 4, 256], F32) for h in range(2)]
+        yi = [held("yi%d" % h, [P, 256, 4], BF16) for h in range(2)]
+        yc = [held("yc%d" % h, [P, 256], U32) for h in range(2)]
+        ys = held("ys", [P, PAIRS], U8)
+        out0v = out_0.rearrange("(p t) m -> p t m", t=4)
+        out1v = out_1[0].rearrange("p m t -> p (m t)").bitcast(I32)
+
+        def finish(h):
+            for u in range(2):
+                lo = 256 * h + 128 * u
+                acc = ps2.tile([P, 4, 128], F32, name="yacc")
+                for t in range(4):
+                    for b in range(2):
+                        cols = slice(512 * b + 128 * t, 512 * b + 128 * t + 128)
+                        nc.tensor.matmul_mx(
+                            out=acc[:, t, :],
+                            lhsT=w3c[:, cols].bitcast(FP4X4),
+                            lhsT_scale=w3s[:, cols],
+                            rhs=zc[b][:, lo : lo + 128].bitcast(FP8X4),
+                            rhs_scale=zs[b][:, lo : lo + 128],
+                            start=(b == 0),
+                            stop=(b == 1),
+                        )
+                for t in range(4):
+                    nc.scalar.activation(
+                        y[h][:, t, 128 * u : 128 * u + 128], acc[:, t, :], ACT.Copy, scale=og_t[:, t : t + 1]
+                    )
+            nc.sync.dma_start(out0v[:, :, 256 * h : 256 * h + 256], y[h][:])
+            nc.vector.tensor_copy(
+                yi[h][:].rearrange("p (c i) t -> p c t i", i=4),
+                y[h][:].rearrange("p t (c i) -> p c t i", i=4),
+            )
+            nc.vector.quantize_mx(
+                out=yc[h][:].bitcast(FP8X4),
+                scales=ys[:, 256 * h : 256 * h + 256],
+                in_=yi[h][:].rearrange("p m t -> p (m t)"),
+            )
+            nc.sync.dma_start(out1v[:, 256 * h : 256 * h + 256], yc[h][:].bitcast(I32))
+
+        round_w1(0, 0, False)
+        make_ctr(0)
+        round_w1(0, 1, True)
+        load_w1(1, 0, "stage4")
+        load_w1(1, 1, "stage0")
+        deal_w2(1)
+        nc.vector.tensor_copy(
+            w3c[:].rearrange("p (a t c i) -> p a c t i", a=2, t=4, i=8),
+            w3raw[:].rearrange("p (a c i t) -> p a c t i", a=2, t=4, i=8),
+        )
+        nc.vector.tensor_copy(
+            w3s[:].rearrange("p (a t c i) -> p a c t i", a=2, t=4, i=16),
+            w3s_raw[:].rearrange("p (a c i t) -> p a c t i", a=2, t=4, i=16),
+        )
+        make_ctr(1)
+        make_ctr(2)
+        for s in range(8):
+            make_att(s)
+            if s < 7:
+                make_z(s, 0, PAIRS)
+            if s + 3 < 8:
+                make_ctr(s + 3)
+            if s < 2:
+                round_w1(1, s, False)
+        quantize_z(0, 0, PAIRS, False)
+        for h in range(2):
+            make_z(7, 256 * h, 256 * h + 256)
+            quantize_z(1, 256 * h, 256 * h + 256, True)
+            finish(h)
+        for q in range(4):
+            queue = nc.sync if q % 2 == 0 else nc.scalar
+            queue.dma_start(
+                out_2[0, 4 * q : 4 * q + 4, :].bitcast(I32), ys[32 * q : 32 * q + 4, :].bitcast(I32)
+            )

@@ -1,6 +1,7 @@
 from contextlib import ExitStack
 
 import concourse.mybir as mybir
+from concourse.masks import make_identity
 
 K, T, S, H, PAIRS, N = 1024, 4096, 1024, 1024, 512, 512
 FLOPS = 2 * (2 * K * H * S + H * N * PAIRS)
@@ -27,49 +28,51 @@ def tile_list_bout_corner_planner_kernel(
     with ExitStack() as ctx:
         keep = ctx.enter_context(tc.tile_pool(name="keep", bufs=1))
         ring = ctx.enter_context(tc.tile_pool(name="ring", bufs=2))
-        ps1 = ctx.enter_context(tc.psum_pool(name="ps1", bufs=6))
-        ps2 = ctx.enter_context(tc.psum_pool(name="ps2", bufs=2))
+        psum = ctx.enter_context(tc.psum_pool(name="psum", bufs=1))
 
         def held(name, shape, dtype, tag=None):
             return keep.tile(shape, dtype, name=name, tag=tag or name, align_bytes=64)
 
+        turns = {}
+
+        def in_turn(name, count):
+            turns[name] = turns.get(name, -1) + 1
+            return "%s%d" % (name, turns[name] % count)
+
+        def bank_for(name, count):
+            return psum.tile([P, 512], F32, name=in_turn(name, count))
+
         offs_t = held("offs_t", [P, S // 16], U16)
         pos1_t = held("pos1_t", [P, PAIRS // 16], U16)
         pos2_t = held("pos2_t", [P, PAIRS // 16], U16)
-        tabw = [held("tabw0", [P, T], U16, "stage1"), held("tabw1", [P, T], U16)]
+        tabw = [held("tabw0", [P, T], U16), held("tabw1", [P, T], U16, "stage2")]
         tabs = held("tabs", [P, T], U8, "stage0")
         vw = [held("vw%d" % a, [P, S], U16) for a in range(2)]
-        vs_packed = held("vs_packed", [P, S], U8, "stage2")
+        vs_packed = held("vs_packed", [P, S], U8, "stage5")
         vs = [held("vs%d" % a, [P, S], U8) for a in range(2)]
         w2raw = {0: held("w2raw0", [P, 2, 512], I32)}
-        w2c = [held("w2c%d" % b, [P, 2, 512], I32) for b in range(2)]
-        w2s_raw = held("w2s_raw", [P, 2 * H], U8, "stage3")
-        w2s = held("w2s", [P, 4, 512], U8)
+        w2s = held("w2s", [P, 2 * H], U8)
+        ident = held("ident", [P, P], F32)
+        vec_rows = held("vec_rows", [P, P], F32, "stage3")
+        vec = held("vec", [P, 16], F32)
         w3c = held("w3c", [P, 2 * N], U16)
-        w3s_raw = held("w3s_raw", [P, 2 * N], U8)
-        w3s = held("w3s", [P, 2 * N], U8)
         w1raw = {}
         w1c = [[held("w1c%d%d" % (b, a), [P, 512], U32) for a in range(2)] for b in range(2)]
         w1s = [[held("w1s%d%d" % (b, a), [P, 512], U8) for a in range(2)] for b in range(2)]
-        bc_t = held("bc_t", [P, 2, 4], F32)
-        cg_t = held("cg_t", [P, 2, 4], F32)
-        og_t = held("og_t", [P, 4], F32)
         warm = held("warm", [P, 8], F32)
         warm_out = held("warm_out", [P, 8], F32)
 
-        nc.vector.memset(w2s_raw[:].bitcast(I32), 0)
-        for q in range(4):
-            (nc.vector if q < 3 else nc.gpsimd).memset(tabs[32 * q : 32 * q + 24, :].bitcast(I32), 0)
         nc.vector.memset(warm[:], 0.0)
+        nc.vector.memset(w2s[:].bitcast(I32), 0)
+        nc.vector.memset(vec_rows[:], 0.0)
+        nc.vector.memset(tabs[0:64, :].bitcast(I32), 0)
+        nc.vector.memset(tabs[64:96, :].bitcast(I32), 0)
         for a in range(2):
-            nc.vector.memset(vs[a][:].bitcast(I32), 0)
+            nc.gpsimd.memset(vs[a][:].bitcast(I32), 0)
+        make_identity(nc, ident[:])
 
         nc.sync.dma_start(offs_t[:], offs)
-        for q in range(4):
-            nc.sync.dma_start(
-                tabs[32 * q + 24 : 32 * q + 32, :].bitcast(I32),
-                tab_scales[:, 4 * q : 4 * q + 4, :].bitcast(I32),
-            )
+        nc.sync.dma_start(tabs[96:P, :].bitcast(I32), tab_scales.rearrange("a q t -> (a q) t").bitcast(I32))
         w2v = w2_words.rearrange("a p c i -> p a (c i)").bitcast(I32)
         w1v = w1.rearrange("(a p j) c -> a p j c", a=2, j=4)
         nc.sync.dma_start(tabw[0][:].bitcast(I32), tab_words[0].bitcast(I32))
@@ -77,65 +80,53 @@ def tile_list_bout_corner_planner_kernel(
         nc.sync.dma_start(pos2_t[:], pos2)
         nc.sync.dma_start(tabw[1][:].bitcast(I32), tab_words[1].bitcast(I32))
 
-        def load_w1(b, a, tag):
-            w1raw[b, a] = held("w1raw%d%d" % (b, a), [P, 4, 512], F32, tag)
-            nc.sync.dma_start(w1raw[b, a][:], w1v[a, :, :, 512 * b : 512 * b + 512])
+        def load_w1(b):
+            w1raw[b] = held("w1raw%d" % b, [P, 2, 4, 512], F32, "stage5")
+            for a in range(2):
+                nc.sync.dma_start(w1raw[b][:, a], w1v[a, :, :, 512 * b : 512 * b + 512])
 
-        load_w1(0, 0, "stage4")
         nc.sync.dma_start(w2raw[0][:], w2v[:, :, 0:512])
         for q in range(4):
             nc.scalar.dma_start(
-                w2s_raw[32 * q : 32 * q + 4, :].bitcast(I32).rearrange("p (a c) -> p a c", a=2),
+                w2s[32 * q : 32 * q + 4, :].bitcast(I32).rearrange("p (a c) -> p a c", a=2),
                 w2_scales[:, 4 * q : 4 * q + 4, :].rearrange("a r c -> r a c").bitcast(I32),
             )
         nc.scalar.activation(warm_out[:], warm[:], ACT.Tanh)
-        nc.gpsimd.dma_start(bc_t[:], bc.rearrange("(b p t) -> p b t", b=2, t=4))
-        nc.gpsimd.dma_start(cg_t[:], cgain.rearrange("(b p t) -> p b t", b=2, t=4))
+        nc.gpsimd.dma_start(vec_rows[0:8, :], bc.rearrange("(s p) -> s p", p=P))
+        nc.gpsimd.dma_start(vec_rows[8:16, :], cgain.rearrange("(s p) -> s p", p=P))
+        vec_ps = bank_for("misc", 2)
+        nc.tensor.transpose(vec_ps[:, 0:P], vec_rows[:], ident[:])
+        nc.vector.tensor_copy(vec[:], vec_ps[:, 0:16])
+        w3s_raw = held("w3s_raw", [P, 2 * N], U8, "stage3")
         nc.gpsimd.memset(w3s_raw[:].bitcast(I32), 0)
         for q in range(4):
             nc.gpsimd.dma_start(
                 w3s_raw[32 * q : 32 * q + 4, :].bitcast(I32).rearrange("p (a c) -> p a c", a=2),
                 w3_scales[:, 4 * q : 4 * q + 4, :].rearrange("a r c -> r a c").bitcast(I32),
             )
-        nc.gpsimd.dma_start(og_t[:], ogain.rearrange("(p t) -> p t", t=4))
 
         nc.vector.tensor_copy(vs_packed[:], tabs[:].indirect(offs_t[:]))
         for a in range(2):
-            first_row = 24 + 4 * a
-            nc.scalar.dma_start(
-                vs[a][0 : P - first_row, :].bitcast(I32), vs_packed[first_row:P, :].bitcast(I32)
-            )
+            for q in range(4):
+                row = 96 + 16 * a + 4 * q
+                nc.scalar.dma_start(
+                    vs[a][32 * q : 32 * q + 4, :].bitcast(I32), vs_packed[row : row + 4, :].bitcast(I32)
+                )
+        gain = held("gain", [P, 8, PAIRS], F32, "stage0")
 
-        load_w1(0, 1, "stage0")
         nc.vector.tensor_copy(vw[0][:], tabw[0][:].indirect(offs_t[:]))
-        w2raw[1] = held("w2raw1", [P, 2, 512], I32, "stage1")
-        nc.sync.dma_start(w2raw[1][:], w2v[:, :, 512:1024])
-        nc.vector.tensor_copy(
-            w2s[:].rearrange("p g (t c i) -> p g c t i", t=4, i=16),
-            w2s_raw[:].rearrange("p (g c i t) -> p g c t i", g=4, t=4, i=16),
-        )
-        w3raw = held("w3raw", [P, 2 * N], U16, "stage2")
-        nc.sync.dma_start(
-            w3raw[:].bitcast(I32).rearrange("p (a c) -> p a c", a=2),
-            w3_words.rearrange("a p c -> p a c").bitcast(I32),
-        )
-
-        def deal_w2(b):
-            nc.vector.tensor_copy(
-                w2c[b][:].rearrange("p a (t c i) -> p a c t i", t=4, i=4),
-                w2raw[b][:].rearrange("p a (c i t) -> p a c t i", t=4, i=4),
-            )
-
-        deal_w2(0)
         for h in range(2):
             nc.vector.tensor_copy(
                 vw[1][:, 512 * h : 512 * h + 512], tabw[1][:].indirect(offs_t[:, 32 * h : 32 * h + 32])
             )
+        load_w1(0)
+        w2raw[1] = held("w2raw1", [P, 2, 512], I32, "stage2")
+        nc.sync.dma_start(w2raw[1][:], w2v[:, :, 512:1024])
 
         def round_w1(b, a, on_vector):
-            grouped = held("w1bf%d%d" % (b, a), [P, 4, 128, 4], BF16, "stage3" if a == 1 else "w1bf")
-            dst = grouped[:].rearrange("p t m j -> p m t j")
-            src = w1raw[b, a][:].rearrange("p j (m t) -> p m t j", t=4)
+            grouped = ring.tile([P, 512, 4], BF16, name="w1bf", align_bytes=64)
+            dst = grouped[:].rearrange("p (c i) j -> p c j i", i=4)
+            src = w1raw[b][:, a].rearrange("p j (c i) -> p c j i", i=4)
             if on_vector:
                 nc.vector.tensor_copy(dst, src)
             else:
@@ -143,11 +134,11 @@ def tile_list_bout_corner_planner_kernel(
             nc.vector.quantize_mx(
                 out=w1c[b][a][:].bitcast(FP8X4),
                 scales=w1s[b][a][:],
-                in_=grouped[:].rearrange("p t m j -> p (t m j)"),
+                in_=grouped[:].rearrange("p c j -> p (c j)"),
             )
 
         def product(codes, scales, h):
-            acc = ps1.tile([P, 512], F32, name="acc")
+            acc = bank_for("acc", 3)
             cols = slice(512 * h, 512 * h + 512)
             for a in range(2):
                 nc.tensor.matmul_mx(
@@ -169,24 +160,24 @@ def tile_list_bout_corner_planner_kernel(
         def make_ctr(s):
             b, t = divmod(s, 4)
             ctr[s] = ring.tile([P, S], F32, name="ctr", bufs=4)
+            nc.scalar.copy(gain[:, s, :], vec[:, 8 + s : 9 + s].to_broadcast([P, PAIRS]))
             for h in range(2):
                 acc = product(
-                    lambda a: w2c[b][:, a, 128 * t : 128 * t + 128],
-                    lambda a: w2s[:, 2 * a + b, 128 * t : 128 * t + 128],
+                    lambda a: w2raw[b][:, a, 128 * t : 128 * t + 128],
+                    lambda a: w2s[:, H * a + 128 * s : H * a + 128 * s + 128],
                     h,
                 )
-                th = ring.tile([P, 512], F32, name="th", bufs=3)
-                nc.scalar.activation(th[:], acc[:], ACT.Tanh, bias=bc_t[:, b, t : t + 1])
                 nc.scalar.activation(
-                    ctr[s][:, 512 * h : 512 * h + 512], th[:], ACT.Copy, scale=cg_t[:, b, t : t + 1]
+                    ctr[s][:, 512 * h : 512 * h + 512], acc[:], ACT.Tanh, bias=vec[:, s : s + 1]
                 )
-            c1[s] = ring.tile([P, PAIRS], F32, name="c1", bufs=6)
-            c2[s] = ring.tile([P, PAIRS], F32, name="c2", bufs=6)
-            nc.vector.tensor_copy(c2[s][:], ctr[s][:].indirect(pos2_t[:]))
-            nc.vector.tensor_copy(c1[s][:], ctr[s][:].indirect(pos1_t[:]))
+            c1[s] = ring.tile([P, PAIRS], F32, name="c1", bufs=8)
+            c2[s] = ring.tile([P, PAIRS], F32, name="c2", bufs=8)
+            nc.vector.tensor_tensor(c2[s][:], ctr[s][:].indirect(pos2_t[:]), gain[:, s, :], ALU.mult)
+            nc.vector.tensor_tensor(c1[s][:], ctr[s][:].indirect(pos1_t[:]), gain[:, s, :], ALU.mult)
 
-        zb = [held("zb%d" % b, [P, 4, PAIRS], BF16) for b in range(2)]
-        zi = [held("zi%d" % b, [P, PAIRS, 4], BF16) for b in range(2)]
+        zt0 = held("zt0", [P, 4, 512], BF16)
+        zt = [[zt0[:, 0:2, :], zt0[:, 2:4, :]], [held("zt1%d" % h, [P, 2, 512], BF16)[:] for h in range(2)]]
+        zi = [[held("zi%d%d" % (b, h), [P, 1024], BF16) for h in range(2)] for b in range(2)]
         zc = [held("zc%d" % b, [P, PAIRS], U32) for b in range(2)]
         zs = [held("zs%d" % b, [P, PAIRS], U8) for b in range(2)]
 
@@ -201,27 +192,75 @@ def tile_list_bout_corner_planner_kernel(
                 )
                 nc.scalar.copy(att[s][:, 512 * h : 512 * h + 512], acc[:])
 
-        def make_z(s, lo, hi):
-            b, t = divmod(s, 4)
-            first = ring.tile([P, hi - lo], F32, name="first")
-            second = ring.tile([P, hi - lo], F32, name="second")
-            o = slice(lo // 16, hi // 16)
-            nc.vector.tensor_tensor(first[:], att[s][:].indirect(pos1_t[:, o]), c2[s][:, lo:hi], ALU.add)
-            nc.vector.tensor_tensor(second[:], att[s][:].indirect(pos2_t[:, o]), c1[s][:, lo:hi], ALU.add)
-            nc.vector.tensor_tensor(zb[b][:, t, lo:hi], first[:], second[:], ALU.max)
+        late = {}
+        a1 = {}
+        a2 = {}
 
-        def quantize_z(b, lo, hi, on_vector):
-            dst = zi[b][:, lo:hi, :].rearrange("p (c i) t -> p c t i", i=4)
-            src = zb[b][:, :, lo:hi].rearrange("p t (c i) -> p c t i", i=4)
-            if on_vector:
-                nc.vector.tensor_copy(dst, src)
+        def pick_att(s, lo, hi):
+            if s == 0:
+                a1[s] = held("a1_0", [P, PAIRS], F32, "stage5")[:]
+                a2[s] = ring.tile([P, PAIRS], F32, name="a2", bufs=3)[:]
+            elif lo == 0:
+                a1[s] = ring.tile([P, hi], F32, name="a1", bufs=3)[:]
+                a2[s] = ring.tile([P, hi], F32, name="a2", bufs=3)[:]
             else:
-                nc.scalar.copy(dst, src)
-            nc.vector.quantize_mx(
-                out=zc[b][:, lo:hi].bitcast(FP8X4),
-                scales=zs[b][:, lo:hi],
-                in_=zi[b][:, lo:hi, :].rearrange("p m t -> p (m t)"),
+                both = held(in_turn("second_sb", 2), [P, 512], F32)
+                a1[s], a2[s] = both[:, 0:256], both[:, 256:512]
+            o = slice(lo // 16, hi // 16)
+            nc.vector.tensor_copy(a2[s], att[s][:].indirect(pos2_t[:, o]))
+            nc.vector.tensor_copy(a1[s], att[s][:].indirect(pos1_t[:, o]))
+
+        def make_z(s, m0, m1):
+            b, t = divmod(s, 4)
+            first = bank_for("first", 2)
+            if m0 == 0:
+                second = bank_for("second", 1)
+            else:
+                second = bank_for("acc", 3)
+            width = 128 * (m1 - m0)
+            blocks = range(m1 - m0)
+            for bank, picked_c, picked_a in ((second, c1[s], a2[s]), (first, c2[s], a1[s])):
+                for g in blocks:
+                    nc.tensor.matmul(
+                        bank[:, 128 * g : 128 * g + 128], picked_c[:, 128 * (m0 + g) : 128 * (m0 + g) + 128],
+                        ident[:], start=(g == 0), stop=False, is_transpose=True,
+                    )
+                for g in blocks:
+                    nc.tensor.matmul(
+                        bank[:, 128 * g : 128 * g + 128], picked_a[:, 128 * g : 128 * g + 128],
+                        ident[:], start=False, stop=(g == blocks[-1]), is_transpose=True,
+                    )
+            second_sb = held(in_turn("second_sb", 2), [P, 512], F32)
+            nc.scalar.copy(second_sb[:, 0:width], second[:, 0:width])
+            if b == 0:
+                parts = [(zt0[:], 0, width)]
+            else:
+                parts = [(zt[1][h], 256 * h - 128 * m0, 256 * h + 256 - 128 * m0) for h in range(m0 // 2, m1 // 2)]
+            for dst, lo, hi in parts:
+                nc.vector.tensor_tensor(
+                    dst[:, :, 128 * t : 128 * t + 128],
+                    first[:, lo:hi].rearrange("p (g r) -> p g r", r=128),
+                    second_sb[:, lo:hi].rearrange("p (g r) -> p g r", r=128),
+                    ALU.max,
+                )
+
+        def quantize_z(b, h):
+            back = bank_for("misc", 2)
+            words = zt[b][h].bitcast(F32)
+            for g in range(2):
+                for u in range(2):
+                    nc.tensor.transpose(
+                        back[:, 256 * g + 128 * u : 256 * g + 128 * u + 128],
+                        words[:, g, u:256:2],
+                        ident[:],
+                    )
+            lo, hi = 256 * h, 256 * h + 256
+            flat = zi[b][h][:]
+            nc.scalar.copy(
+                flat.bitcast(F32).rearrange("p (g m u) -> p g m u", g=2, u=2),
+                back[:].rearrange("p (g u m) -> p g m u", g=2, u=2),
             )
+            nc.vector.quantize_mx(out=zc[b][:, lo:hi].bitcast(FP8X4), scales=zs[b][:, lo:hi], in_=flat)
 
         y = [held("y%d" % h, [P, 4, 256], F32) for h in range(2)]
         yi = [held("yi%d" % h, [P, 256, 4], BF16) for h in range(2)]
@@ -230,25 +269,39 @@ def tile_list_bout_corner_planner_kernel(
         out0v = out_0.rearrange("(p t) m -> p t m", t=4)
         out1v = out_1[0].rearrange("p m t -> p (m t)").bitcast(I32)
 
+        ybank = {}
+
+        def last_product(quarter, b):
+            lo = 128 * quarter
+            for t in range(4):
+                cols = slice(512 * b + 128 * t, 512 * b + 128 * t + 128)
+                nc.tensor.matmul_mx(
+                    out=ybank[quarter][:, 128 * t : 128 * t + 128],
+                    lhsT=w3c[:, cols].bitcast(FP4X4),
+                    lhsT_scale=late["w3s"][:, cols],
+                    rhs=zc[b][:, lo : lo + 128].bitcast(FP8X4),
+                    rhs_scale=zs[b][:, lo : lo + 128],
+                    start=(b == 0 and t == 0),
+                    stop=(b == 1 and t == 3),
+                )
+
         def finish(h):
+            og_t = late["og"]
             for u in range(2):
-                lo = 256 * h + 128 * u
-                acc = ps2.tile([P, 4, 128], F32, name="yacc")
-                for t in range(4):
-                    for b in range(2):
-                        cols = slice(512 * b + 128 * t, 512 * b + 128 * t + 128)
-                        nc.tensor.matmul_mx(
-                            out=acc[:, t, :],
-                            lhsT=w3c[:, cols].bitcast(FP4X4),
-                            lhsT_scale=w3s[:, cols],
-                            rhs=zc[b][:, lo : lo + 128].bitcast(FP8X4),
-                            rhs_scale=zs[b][:, lo : lo + 128],
-                            start=(b == 0),
-                            stop=(b == 1),
+                acc = ybank[2 * h + u]
+                last_product(2 * h + u, 1)
+                if u == 0:
+                    for t in range(4):
+                        nc.scalar.activation(
+                            y[h][:, t, 0:128], acc[:, 128 * t : 128 * t + 128], ACT.Copy,
+                            scale=og_t[:, t : t + 1],
                         )
-                for t in range(4):
-                    nc.scalar.activation(
-                        y[h][:, t, 128 * u : 128 * u + 128], acc[:, t, :], ACT.Copy, scale=og_t[:, t : t + 1]
+                else:
+                    nc.vector.tensor_tensor(
+                        y[h][:, :, 128:256],
+                        acc[:].rearrange("p (t m) -> p t m", t=4),
+                        og_t[:].unsqueeze(2).to_broadcast([P, 4, 128]),
+                        ALU.mult,
                     )
             nc.sync.dma_start(out0v[:, :, 256 * h : 256 * h + 256], y[h][:])
             nc.vector.tensor_copy(
@@ -262,34 +315,59 @@ def tile_list_bout_corner_planner_kernel(
             )
             nc.sync.dma_start(out1v[:, 256 * h : 256 * h + 256], yc[h][:].bitcast(I32))
 
+        def deal_w3():
+            w3s = late["w3s"] = held("w3s", [P, 2 * N], U8, "stage2")
+            w3raw = held("w3raw", [P, 2 * N], U16, "stage5")
+            nc.sync.dma_start(
+                w3raw[:].bitcast(I32).rearrange("p (a c) -> p a c", a=2),
+                w3_words.rearrange("a p c -> p a c").bitcast(I32),
+            )
+            nc.vector.tensor_copy(
+                w3c[:].rearrange("p (a t c i) -> p a c t i", a=2, t=4, i=8),
+                w3raw[:].rearrange("p (a c i t) -> p a c t i", a=2, t=4, i=8),
+            )
+            nc.vector.tensor_copy(
+                w3s[:].rearrange("p (a t c i) -> p a c t i", a=2, t=4, i=16),
+                w3s_raw[:].rearrange("p (a c i t) -> p a c t i", a=2, t=4, i=16),
+            )
+            late["og"] = held("og_t", [P, 4], F32, "stage3")
+            nc.sync.dma_start(late["og"][:], ogain.rearrange("(p t) -> p t", t=4))
+
+        for s in range(3):
+            make_ctr(s)
         round_w1(0, 0, False)
-        make_ctr(0)
-        round_w1(0, 1, True)
-        load_w1(1, 0, "stage4")
-        load_w1(1, 1, "stage0")
-        deal_w2(1)
-        nc.vector.tensor_copy(
-            w3c[:].rearrange("p (a t c i) -> p a c t i", a=2, t=4, i=8),
-            w3raw[:].rearrange("p (a c i t) -> p a c t i", a=2, t=4, i=8),
-        )
-        nc.vector.tensor_copy(
-            w3s[:].rearrange("p (a t c i) -> p a c t i", a=2, t=4, i=16),
-            w3s_raw[:].rearrange("p (a c i t) -> p a c t i", a=2, t=4, i=16),
-        )
-        make_ctr(1)
-        make_ctr(2)
+        make_ctr(3)
+        round_w1(0, 1, False)
+        make_ctr(4)
         for s in range(8):
             make_att(s)
             if s < 7:
-                make_z(s, 0, PAIRS)
-            if s + 3 < 8:
-                make_ctr(s + 3)
-            if s < 2:
-                round_w1(1, s, False)
-        quantize_z(0, 0, PAIRS, False)
+                pick_att(s, 0, PAIRS)
+            if s > 0:
+                make_z(s - 1, 0, 4)
+            if s == 1:
+                load_w1(1)
+            if s in (2, 3):
+                round_w1(1, s - 2, False)
+            if s + 5 < 8:
+                make_ctr(s + 5)
+            if s == 4:
+                deal_w3()
+            if s in (4, 5):
+                quantize_z(0, s - 4)
+        pick_att(7, 0, 256)
+        make_z(7, 0, 2)
+        pick_att(7, 256, 512)
+        make_z(7, 2, 4)
         for h in range(2):
-            make_z(7, 256 * h, 256 * h + 256)
-            quantize_z(1, 256 * h, 256 * h + 256, True)
+            quantize_z(1, h)
+        ybank[2] = bank_for("acc", 3)
+        ybank[3] = bank_for("acc", 3)
+        ybank[0] = bank_for("second", 1)
+        ybank[1] = bank_for("first", 2)
+        for quarter in (2, 3, 0, 1):
+            last_product(quarter, 0)
+        for h in range(2):
             finish(h)
         for q in range(4):
             queue = nc.sync if q % 2 == 0 else nc.scalar

@@ -45,15 +45,15 @@ def tile_list_bout_corner_planner_kernel(
         offs_t = held("offs_t", [P, S // 16], U16)
         pos1_t = held("pos1_t", [P, PAIRS // 16], U16)
         pos2_t = held("pos2_t", [P, PAIRS // 16], U16)
-        tabw = [held("tabw0", [P, T], U16), held("tabw1", [P, T], U16, "stage2")]
-        tabs = held("tabs", [P, T], U8, "stage0")
+        tabw = [held("tabw0", [P, T], U16, "stage1"), held("tabw1", [P, T], U16, "stage2")]
+        tabs = held("tabs", [P, T], U8)
         vw = [held("vw%d" % a, [P, S], U16) for a in range(2)]
         vs_packed = held("vs_packed", [P, S], U8, "stage5")
         vs = [held("vs%d" % a, [P, S], U8) for a in range(2)]
         w2raw = {0: held("w2raw0", [P, 2, 512], I32)}
         w2s = held("w2s", [P, 2 * H], U8)
         ident = held("ident", [P, P], F32)
-        vec_rows = held("vec_rows", [P, P], F32, "stage3")
+        vec_rows = held("vec_rows", [P, P], F32)
         vec = held("vec", [P, 16], F32)
         w3c = held("w3c", [P, 2 * N], U16)
         w1raw = {}
@@ -64,15 +64,18 @@ def tile_list_bout_corner_planner_kernel(
 
         nc.vector.memset(warm[:], 0.0)
         nc.vector.memset(w2s[:].bitcast(I32), 0)
-        nc.vector.memset(vec_rows[:], 0.0)
+        nc.vector.memset(vec_rows[0:64, :], 0.0)
+        nc.vector.memset(vec_rows[64:112, :], 0.0)
         nc.vector.memset(tabs[0:64, :].bitcast(I32), 0)
         nc.vector.memset(tabs[64:96, :].bitcast(I32), 0)
-        for a in range(2):
-            nc.gpsimd.memset(vs[a][:].bitcast(I32), 0)
         make_identity(nc, ident[:])
+        for a in range(2):
+            nc.vector.memset(vs[a][:].bitcast(I32), 0)
 
         nc.sync.dma_start(offs_t[:], offs)
         nc.sync.dma_start(tabs[96:P, :].bitcast(I32), tab_scales.rearrange("a q t -> (a q) t").bitcast(I32))
+        nc.sync.dma_start(vec_rows[112:120, :], bc.rearrange("(s p) -> s p", p=P))
+        nc.sync.dma_start(vec_rows[120:128, :], cgain.rearrange("(s p) -> s p", p=P))
         w2v = w2_words.rearrange("a p c i -> p a (c i)").bitcast(I32)
         w1v = w1.rearrange("(a p j) c -> a p j c", a=2, j=4)
         nc.sync.dma_start(tabw[0][:].bitcast(I32), tab_words[0].bitcast(I32))
@@ -87,16 +90,14 @@ def tile_list_bout_corner_planner_kernel(
 
         nc.sync.dma_start(w2raw[0][:], w2v[:, :, 0:512])
         for q in range(4):
-            nc.scalar.dma_start(
+            nc.gpsimd.dma_start(
                 w2s[32 * q : 32 * q + 4, :].bitcast(I32).rearrange("p (a c) -> p a c", a=2),
                 w2_scales[:, 4 * q : 4 * q + 4, :].rearrange("a r c -> r a c").bitcast(I32),
             )
         nc.scalar.activation(warm_out[:], warm[:], ACT.Tanh)
-        nc.gpsimd.dma_start(vec_rows[0:8, :], bc.rearrange("(s p) -> s p", p=P))
-        nc.gpsimd.dma_start(vec_rows[8:16, :], cgain.rearrange("(s p) -> s p", p=P))
         vec_ps = bank_for("misc", 2)
         nc.tensor.transpose(vec_ps[:, 0:P], vec_rows[:], ident[:])
-        nc.vector.tensor_copy(vec[:], vec_ps[:, 0:16])
+        nc.scalar.copy(vec[:], vec_ps[:, 112:128])
         w3s_raw = held("w3s_raw", [P, 2 * N], U8, "stage3")
         nc.gpsimd.memset(w3s_raw[:].bitcast(I32), 0)
         for q in range(4):
@@ -109,10 +110,10 @@ def tile_list_bout_corner_planner_kernel(
         for a in range(2):
             for q in range(4):
                 row = 96 + 16 * a + 4 * q
-                nc.scalar.dma_start(
+                nc.sync.dma_start(
                     vs[a][32 * q : 32 * q + 4, :].bitcast(I32), vs_packed[row : row + 4, :].bitcast(I32)
                 )
-        gain = held("gain", [P, 8, PAIRS], F32, "stage0")
+        gain = held("gain", [P, 8, PAIRS], F32)
 
         nc.vector.tensor_copy(vw[0][:], tabw[0][:].indirect(offs_t[:]))
         for h in range(2):
@@ -120,8 +121,8 @@ def tile_list_bout_corner_planner_kernel(
                 vw[1][:, 512 * h : 512 * h + 512], tabw[1][:].indirect(offs_t[:, 32 * h : 32 * h + 32])
             )
         load_w1(0)
-        w2raw[1] = held("w2raw1", [P, 2, 512], I32, "stage2")
-        nc.sync.dma_start(w2raw[1][:], w2v[:, :, 512:1024])
+        w2raw[1] = held("w2raw1", [P, 2, 512], I32, "stage1")
+        nc.scalar.dma_start(w2raw[1][:], w2v[:, :, 512:1024])
 
         def round_w1(b, a, on_vector):
             grouped = ring.tile([P, 512, 4], BF16, name="w1bf", align_bytes=64)
@@ -316,9 +317,9 @@ def tile_list_bout_corner_planner_kernel(
             nc.sync.dma_start(out1v[:, 256 * h : 256 * h + 256], yc[h][:].bitcast(I32))
 
         def deal_w3():
-            w3s = late["w3s"] = held("w3s", [P, 2 * N], U8, "stage2")
-            w3raw = held("w3raw", [P, 2 * N], U16, "stage5")
-            nc.sync.dma_start(
+            w3s = late["w3s"] = held("w3s", [P, 2 * N], U8)
+            w3raw = held("w3raw", [P, 2 * N], U16, "stage2")
+            nc.scalar.dma_start(
                 w3raw[:].bitcast(I32).rearrange("p (a c) -> p a c", a=2),
                 w3_words.rearrange("a p c -> p a c").bitcast(I32),
             )
@@ -335,6 +336,7 @@ def tile_list_bout_corner_planner_kernel(
 
         for s in range(3):
             make_ctr(s)
+        deal_w3()
         round_w1(0, 0, False)
         make_ctr(3)
         round_w1(0, 1, False)
@@ -351,8 +353,6 @@ def tile_list_bout_corner_planner_kernel(
                 round_w1(1, s - 2, False)
             if s + 5 < 8:
                 make_ctr(s + 5)
-            if s == 4:
-                deal_w3()
             if s in (4, 5):
                 quantize_z(0, s - 4)
         pick_att(7, 0, 256)

@@ -18,6 +18,12 @@ ACT = mybir.ActivationFunctionType
 ALU = mybir.AluOpType
 
 P = 128
+BANK = 512
+SLICES = H // P
+HALF = PAIRS // 2
+CTR_LEAD = 5
+SCALE_ROW0 = 96
+VEC_ROW0 = 112
 
 
 def tile_list_bout_corner_planner_kernel(
@@ -39,338 +45,334 @@ def tile_list_bout_corner_planner_kernel(
             turns[name] = turns.get(name, -1) + 1
             return "%s%d" % (name, turns[name] % count)
 
-        def bank_for(name, count):
-            return psum.tile([P, 512], F32, name=in_turn(name, count))
+        bank_counts = {"product": 3, "first": 2, "second": 1, "turned": 2}
+
+        def bank(role):
+            return psum.tile([P, BANK], F32, name=in_turn(role, bank_counts[role]))
 
         offs_t = held("offs_t", [P, S // 16], U16)
         pos1_t = held("pos1_t", [P, PAIRS // 16], U16)
         pos2_t = held("pos2_t", [P, PAIRS // 16], U16)
-        tabw = [held("tabw0", [P, T], U16, "stage1"), held("tabw1", [P, T], U16, "stage2")]
-        tabs = held("tabs", [P, T], U8)
-        vw = [held("vw%d" % a, [P, S], U16) for a in range(2)]
-        vs_packed = held("vs_packed", [P, S], U8, "stage5")
-        vs = [held("vs%d" % a, [P, S], U8) for a in range(2)]
-        w2raw = {0: held("w2raw0", [P, 2, 512], I32)}
-        w2s = held("w2s", [P, 2 * H], U8)
+        tab_w = [held("tab_w%d" % a, [P, T], U16, "table%d" % a) for a in range(2)]
+        tab_s = held("tab_s", [P, T], U8)
+        v_w = [held("v_w%d" % a, [P, S], U16) for a in range(2)]
+        v_s_rows = held("v_s_rows", [P, S], U8, "late_weights")
+        v_s = [held("v_s%d" % a, [P, S], U8) for a in range(2)]
+        w2_first = held("w2_first", [P, 2, BANK], I32)
+        w2_s = held("w2_s", [P, 2 * H], U8)
+        w3_s_raw = held("w3_s_raw", [P, 2 * N], U8, "w3_scales_then_ogain")
+        w3_w = held("w3_w", [P, 2 * N], U16)
+        w3_s = held("w3_s", [P, 2 * N], U8)
+        w1_w = [[held("w1_w%d%d" % (b, a), [P, BANK], U32) for a in range(2)] for b in range(2)]
+        w1_s = [[held("w1_s%d%d" % (b, a), [P, BANK], U8) for a in range(2)] for b in range(2)]
         ident = held("ident", [P, P], F32)
         vec_rows = held("vec_rows", [P, P], F32)
-        vec = held("vec", [P, 16], F32)
-        w3c = held("w3c", [P, 2 * N], U16)
-        w1raw = {}
-        w1c = [[held("w1c%d%d" % (b, a), [P, 512], U32) for a in range(2)] for b in range(2)]
-        w1s = [[held("w1s%d%d" % (b, a), [P, 512], U8) for a in range(2)] for b in range(2)]
-        warm = held("warm", [P, 8], F32)
-        warm_out = held("warm_out", [P, 8], F32)
+        vec = held("vec", [P, 2 * SLICES], F32)
+        gain = held("gain", [P, SLICES, PAIRS], F32)
 
-        nc.vector.memset(warm[:], 0.0)
-        nc.vector.memset(w2s[:].bitcast(I32), 0)
+        nc.vector.memset(w2_s[:].bitcast(I32), 0)
         nc.vector.memset(vec_rows[0:64, :], 0.0)
-        nc.vector.memset(vec_rows[64:112, :], 0.0)
-        nc.vector.memset(tabs[0:64, :].bitcast(I32), 0)
-        nc.vector.memset(tabs[64:96, :].bitcast(I32), 0)
+        nc.vector.memset(vec_rows[64:VEC_ROW0, :], 0.0)
+        nc.vector.memset(tab_s[0:64, :].bitcast(I32), 0)
+        nc.vector.memset(tab_s[64:SCALE_ROW0, :].bitcast(I32), 0)
         make_identity(nc, ident[:])
         for a in range(2):
-            nc.vector.memset(vs[a][:].bitcast(I32), 0)
+            nc.vector.memset(v_s[a][:].bitcast(I32), 0)
 
+        w2_view = w2_words.rearrange("a p c i -> p a (c i)").bitcast(I32)
+        w1_view = w1.rearrange("(a p j) c -> a p j c", a=2, j=4)
         nc.sync.dma_start(offs_t[:], offs)
-        nc.sync.dma_start(tabs[96:P, :].bitcast(I32), tab_scales.rearrange("a q t -> (a q) t").bitcast(I32))
-        nc.sync.dma_start(vec_rows[112:120, :], bc.rearrange("(s p) -> s p", p=P))
-        nc.sync.dma_start(vec_rows[120:128, :], cgain.rearrange("(s p) -> s p", p=P))
-        w2v = w2_words.rearrange("a p c i -> p a (c i)").bitcast(I32)
-        w1v = w1.rearrange("(a p j) c -> a p j c", a=2, j=4)
-        nc.sync.dma_start(tabw[0][:].bitcast(I32), tab_words[0].bitcast(I32))
+        nc.sync.dma_start(
+            tab_s[SCALE_ROW0:P, :].bitcast(I32), tab_scales.rearrange("a q t -> (a q) t").bitcast(I32)
+        )
+        nc.sync.dma_start(vec_rows[VEC_ROW0 : VEC_ROW0 + SLICES, :], bc.rearrange("(s p) -> s p", p=P))
+        nc.sync.dma_start(vec_rows[VEC_ROW0 + SLICES : P, :], cgain.rearrange("(s p) -> s p", p=P))
+        nc.sync.dma_start(tab_w[0][:].bitcast(I32), tab_words[0].bitcast(I32))
         nc.sync.dma_start(pos1_t[:], pos1)
         nc.sync.dma_start(pos2_t[:], pos2)
-        nc.sync.dma_start(tabw[1][:].bitcast(I32), tab_words[1].bitcast(I32))
+        nc.sync.dma_start(tab_w[1][:].bitcast(I32), tab_words[1].bitcast(I32))
+        nc.sync.dma_start(w2_first[:], w2_view[:, :, 0:BANK])
 
-        def load_w1(b):
-            w1raw[b] = held("w1raw%d" % b, [P, 2, 4, 512], F32, "stage5")
-            for a in range(2):
-                nc.sync.dma_start(w1raw[b][:, a], w1v[a, :, :, 512 * b : 512 * b + 512])
+        def load_scale_rows(tile, scales):
+            for q in range(4):
+                nc.gpsimd.dma_start(
+                    tile[32 * q : 32 * q + 4, :].bitcast(I32).rearrange("p (a c) -> p a c", a=2),
+                    scales[:, 4 * q : 4 * q + 4, :].rearrange("a r c -> r a c").bitcast(I32),
+                )
 
-        nc.sync.dma_start(w2raw[0][:], w2v[:, :, 0:512])
-        for q in range(4):
-            nc.gpsimd.dma_start(
-                w2s[32 * q : 32 * q + 4, :].bitcast(I32).rearrange("p (a c) -> p a c", a=2),
-                w2_scales[:, 4 * q : 4 * q + 4, :].rearrange("a r c -> r a c").bitcast(I32),
-            )
-        nc.scalar.activation(warm_out[:], warm[:], ACT.Tanh)
-        vec_ps = bank_for("misc", 2)
-        nc.tensor.transpose(vec_ps[:, 0:P], vec_rows[:], ident[:])
-        nc.scalar.copy(vec[:], vec_ps[:, 112:128])
-        w3s_raw = held("w3s_raw", [P, 2 * N], U8, "stage3")
-        nc.gpsimd.memset(w3s_raw[:].bitcast(I32), 0)
-        for q in range(4):
-            nc.gpsimd.dma_start(
-                w3s_raw[32 * q : 32 * q + 4, :].bitcast(I32).rearrange("p (a c) -> p a c", a=2),
-                w3_scales[:, 4 * q : 4 * q + 4, :].rearrange("a r c -> r a c").bitcast(I32),
-            )
+        load_scale_rows(w2_s, w2_scales)
 
-        nc.vector.tensor_copy(vs_packed[:], tabs[:].indirect(offs_t[:]))
+        vec_bank = bank("turned")
+        nc.tensor.transpose(vec_bank[:, 0:P], vec_rows[:], ident[:])
+        nc.scalar.copy(vec[:], vec_bank[:, VEC_ROW0:P])
+        nc.gpsimd.memset(w3_s_raw[:].bitcast(I32), 0)
+        load_scale_rows(w3_s_raw, w3_scales)
+
+        nc.vector.tensor_copy(v_s_rows[:], tab_s[:].indirect(offs_t[:]))
         for a in range(2):
             for q in range(4):
-                row = 96 + 16 * a + 4 * q
+                row = SCALE_ROW0 + 16 * a + 4 * q
                 nc.sync.dma_start(
-                    vs[a][32 * q : 32 * q + 4, :].bitcast(I32), vs_packed[row : row + 4, :].bitcast(I32)
+                    v_s[a][32 * q : 32 * q + 4, :].bitcast(I32), v_s_rows[row : row + 4, :].bitcast(I32)
                 )
-        gain = held("gain", [P, 8, PAIRS], F32)
-
-        nc.vector.tensor_copy(vw[0][:], tabw[0][:].indirect(offs_t[:]))
+        nc.vector.tensor_copy(v_w[0][:], tab_w[0][:].indirect(offs_t[:]))
         for h in range(2):
             nc.vector.tensor_copy(
-                vw[1][:, 512 * h : 512 * h + 512], tabw[1][:].indirect(offs_t[:, 32 * h : 32 * h + 32])
+                v_w[1][:, BANK * h : BANK * (h + 1)], tab_w[1][:].indirect(offs_t[:, 32 * h : 32 * (h + 1)])
             )
-        load_w1(0)
-        w2raw[1] = held("w2raw1", [P, 2, 512], I32, "stage1")
-        nc.scalar.dma_start(w2raw[1][:], w2v[:, :, 512:1024])
 
-        def round_w1(b, a, on_vector):
-            grouped = ring.tile([P, 512, 4], BF16, name="w1bf", align_bytes=64)
-            dst = grouped[:].rearrange("p (c i) j -> p c j i", i=4)
-            src = w1raw[b][:, a].rearrange("p j (c i) -> p c j i", i=4)
-            if on_vector:
-                nc.vector.tensor_copy(dst, src)
-            else:
-                nc.scalar.copy(dst, src)
+        w1_cols = 4 * BANK
+        w1_first = held("w1_first", [P, 2 * w1_cols], F32, "late_weights")
+        w1_raw = {(0, a): w1_first[:, w1_cols * a : w1_cols * (a + 1)] for a in range(2)}
+        packed_in = held("packed_in", [P, 2 * BANK + N], I32, "table1")
+        w2_second = packed_in[:, 0 : 2 * BANK]
+        w3_raw = packed_in[:, 2 * BANK : 2 * BANK + N]
+        w2_w = [w2_first[:], w2_second.rearrange("p (a c) -> p a c", a=2)]
+
+        def w1_rows(b, a):
+            return w1_raw[b, a].rearrange("p (j c) -> p j c", j=4)
+
+        def load_w1(b, a):
+            nc.sync.dma_start(w1_rows(b, a), w1_view[a, :, :, BANK * b : BANK * (b + 1)])
+
+        nc.sync.dma_start(
+            w3_raw.rearrange("p (a c) -> p a c", a=2), w3_words.rearrange("a p c -> p a c").bitcast(I32)
+        )
+        load_w1(0, 0)
+        nc.sync.dma_start(w2_w[1], w2_view[:, :, BANK : 2 * BANK])
+        load_w1(0, 1)
+
+        def quantize_w1(b, a):
+            grouped = held("w1_grouped%d%d" % (b, a), [P, BANK, 4], BF16, "w1_next%d" % a if b == 0 else None)
+            nc.scalar.copy(
+                grouped[:].rearrange("p (c i) j -> p c j i", i=4),
+                w1_rows(b, a).rearrange("p j (c i) -> p c j i", i=4),
+            )
             nc.vector.quantize_mx(
-                out=w1c[b][a][:].bitcast(FP8X4),
-                scales=w1s[b][a][:],
+                out=w1_w[b][a][:].bitcast(FP8X4),
+                scales=w1_s[b][a][:],
                 in_=grouped[:].rearrange("p c j -> p (c j)"),
             )
 
-        def product(codes, scales, h):
-            acc = bank_for("acc", 3)
-            cols = slice(512 * h, 512 * h + 512)
+        def first_product(words, scales, h):
+            acc = bank("product")
+            cols = slice(BANK * h, BANK * (h + 1))
             for a in range(2):
                 nc.tensor.matmul_mx(
                     out=acc[:],
-                    lhsT=codes(a).bitcast(FP8X4),
-                    lhsT_scale=scales(a),
-                    rhs=vw[a][:, cols].bitcast(FP4X4),
-                    rhs_scale=vs[a][:, cols],
+                    lhsT=words[a].bitcast(FP8X4),
+                    lhsT_scale=scales[a],
+                    rhs=v_w[a][:, cols].bitcast(FP4X4),
+                    rhs_scale=v_s[a][:, cols],
                     start=(a == 0),
                     stop=(a == 1),
                 )
             return acc
 
-        ctr = {}
-        att = {}
-        c1 = {}
-        c2 = {}
+        att, att1, att2, ctr1, ctr2 = {}, {}, {}, {}, {}
 
-        def make_ctr(s):
+        def pick_ctr(s):
             b, t = divmod(s, 4)
-            ctr[s] = ring.tile([P, S], F32, name="ctr", bufs=4)
-            nc.scalar.copy(gain[:, s, :], vec[:, 8 + s : 9 + s].to_broadcast([P, PAIRS]))
+            bounded = ring.tile([P, S], F32, name="bounded", bufs=4)
+            nc.scalar.copy(gain[:, s, :], vec[:, SLICES + s : SLICES + s + 1].to_broadcast([P, PAIRS]))
             for h in range(2):
-                acc = product(
-                    lambda a: w2raw[b][:, a, 128 * t : 128 * t + 128],
-                    lambda a: w2s[:, H * a + 128 * s : H * a + 128 * s + 128],
+                acc = first_product(
+                    [w2_w[b][:, a, P * t : P * (t + 1)] for a in range(2)],
+                    [w2_s[:, H * a + P * s : H * a + P * (s + 1)] for a in range(2)],
                     h,
                 )
                 nc.scalar.activation(
-                    ctr[s][:, 512 * h : 512 * h + 512], acc[:], ACT.Tanh, bias=vec[:, s : s + 1]
+                    bounded[:, BANK * h : BANK * (h + 1)], acc[:], ACT.Tanh, bias=vec[:, s : s + 1]
                 )
-            c1[s] = ring.tile([P, PAIRS], F32, name="c1", bufs=8)
-            c2[s] = ring.tile([P, PAIRS], F32, name="c2", bufs=8)
-            nc.vector.tensor_tensor(c2[s][:], ctr[s][:].indirect(pos2_t[:]), gain[:, s, :], ALU.mult)
-            nc.vector.tensor_tensor(c1[s][:], ctr[s][:].indirect(pos1_t[:]), gain[:, s, :], ALU.mult)
-
-        zt0 = held("zt0", [P, 4, 512], BF16)
-        zt = [[zt0[:, 0:2, :], zt0[:, 2:4, :]], [held("zt1%d" % h, [P, 2, 512], BF16)[:] for h in range(2)]]
-        zi = [[held("zi%d%d" % (b, h), [P, 1024], BF16) for h in range(2)] for b in range(2)]
-        zc = [held("zc%d" % b, [P, PAIRS], U32) for b in range(2)]
-        zs = [held("zs%d" % b, [P, PAIRS], U8) for b in range(2)]
+            ctr1[s] = ring.tile([P, PAIRS], F32, name="ctr1", bufs=SLICES)
+            ctr2[s] = ring.tile([P, PAIRS], F32, name="ctr2", bufs=SLICES)
+            nc.vector.tensor_tensor(ctr2[s][:], bounded[:].indirect(pos2_t[:]), gain[:, s, :], ALU.mult)
+            nc.vector.tensor_tensor(ctr1[s][:], bounded[:].indirect(pos1_t[:]), gain[:, s, :], ALU.mult)
 
         def make_att(s):
             b, t = divmod(s, 4)
             att[s] = ring.tile([P, S], F32, name="att", bufs=4)
             for h in range(2):
-                acc = product(
-                    lambda a: w1c[b][a][:, 128 * t : 128 * t + 128],
-                    lambda a: w1s[b][a][:, 128 * t : 128 * t + 128],
+                acc = first_product(
+                    [w1_w[b][a][:, P * t : P * (t + 1)] for a in range(2)],
+                    [w1_s[b][a][:, P * t : P * (t + 1)] for a in range(2)],
                     h,
                 )
-                nc.scalar.copy(att[s][:, 512 * h : 512 * h + 512], acc[:])
-
-        late = {}
-        a1 = {}
-        a2 = {}
+                nc.scalar.copy(att[s][:, BANK * h : BANK * (h + 1)], acc[:])
 
         def pick_att(s, lo, hi):
-            if s == 0:
-                a1[s] = held("a1_0", [P, PAIRS], F32, "stage5")[:]
-                a2[s] = ring.tile([P, PAIRS], F32, name="a2", bufs=3)[:]
-            elif lo == 0:
-                a1[s] = ring.tile([P, hi], F32, name="a1", bufs=3)[:]
-                a2[s] = ring.tile([P, hi], F32, name="a2", bufs=3)[:]
+            if lo == 0:
+                att1[s] = ring.tile([P, hi], F32, name="att1", bufs=3)[:]
+                att2[s] = ring.tile([P, hi], F32, name="att2", bufs=3)[:]
             else:
-                both = held(in_turn("second_sb", 2), [P, 512], F32)
-                a1[s], a2[s] = both[:, 0:256], both[:, 256:512]
-            o = slice(lo // 16, hi // 16)
-            nc.vector.tensor_copy(a2[s], att[s][:].indirect(pos2_t[:, o]))
-            nc.vector.tensor_copy(a1[s], att[s][:].indirect(pos1_t[:, o]))
+                both = held(in_turn("second_sb", 2), [P, BANK], F32)
+                att1[s], att2[s] = both[:, 0:HALF], both[:, HALF:BANK]
+            entries = slice(lo // 16, hi // 16)
+            nc.vector.tensor_copy(att2[s], att[s][:].indirect(pos2_t[:, entries]))
+            nc.vector.tensor_copy(att1[s], att[s][:].indirect(pos1_t[:, entries]))
 
-        def make_z(s, m0, m1):
+        z_t0 = held("z_t0", [P, 4, BANK], BF16)
+        z_t = [
+            [z_t0[:, 0:2, :], z_t0[:, 2:4, :]],
+            [held("z_t1%d" % h, [P, 2, BANK], BF16)[:] for h in range(2)],
+        ]
+        z_grouped = [[held("z_grouped%d%d" % (b, h), [P, 4 * HALF], BF16) for h in range(2)] for b in range(2)]
+        z_w = [held("z_w%d" % b, [P, PAIRS], U32) for b in range(2)]
+        z_s = [held("z_s%d" % b, [P, PAIRS], U8) for b in range(2)]
+
+        def make_z(s, lo, hi):
             b, t = divmod(s, 4)
-            first = bank_for("first", 2)
-            if m0 == 0:
-                second = bank_for("second", 1)
-            else:
-                second = bank_for("acc", 3)
-            width = 128 * (m1 - m0)
-            blocks = range(m1 - m0)
-            for bank, picked_c, picked_a in ((second, c1[s], a2[s]), (first, c2[s], a1[s])):
+            first = bank("first")
+            second = bank("second" if lo == 0 else "product")
+            width = hi - lo
+            blocks = range(width // P)
+            for acc, picked_ctr, picked_att in ((second, ctr1[s], att2[s]), (first, ctr2[s], att1[s])):
                 for g in blocks:
                     nc.tensor.matmul(
-                        bank[:, 128 * g : 128 * g + 128], picked_c[:, 128 * (m0 + g) : 128 * (m0 + g) + 128],
+                        acc[:, P * g : P * (g + 1)], picked_ctr[:, lo + P * g : lo + P * (g + 1)],
                         ident[:], start=(g == 0), stop=False, is_transpose=True,
                     )
                 for g in blocks:
                     nc.tensor.matmul(
-                        bank[:, 128 * g : 128 * g + 128], picked_a[:, 128 * g : 128 * g + 128],
+                        acc[:, P * g : P * (g + 1)], picked_att[:, P * g : P * (g + 1)],
                         ident[:], start=False, stop=(g == blocks[-1]), is_transpose=True,
                     )
-            second_sb = held(in_turn("second_sb", 2), [P, 512], F32)
+            second_sb = held(in_turn("second_sb", 2), [P, BANK], F32)
             nc.scalar.copy(second_sb[:, 0:width], second[:, 0:width])
             if b == 0:
-                parts = [(zt0[:], 0, width)]
+                parts = [(z_t0[:], slice(0, width))]
             else:
-                parts = [(zt[1][h], 256 * h - 128 * m0, 256 * h + 256 - 128 * m0) for h in range(m0 // 2, m1 // 2)]
-            for dst, lo, hi in parts:
+                parts = [
+                    (z_t[1][h], slice(HALF * h - lo, HALF * (h + 1) - lo))
+                    for h in range(lo // HALF, hi // HALF)
+                ]
+            for dst, cols in parts:
                 nc.vector.tensor_tensor(
-                    dst[:, :, 128 * t : 128 * t + 128],
-                    first[:, lo:hi].rearrange("p (g r) -> p g r", r=128),
-                    second_sb[:, lo:hi].rearrange("p (g r) -> p g r", r=128),
+                    dst[:, :, P * t : P * (t + 1)],
+                    first[:, cols].rearrange("p (g r) -> p g r", r=P),
+                    second_sb[:, cols].rearrange("p (g r) -> p g r", r=P),
                     ALU.max,
                 )
 
         def quantize_z(b, h):
-            back = bank_for("misc", 2)
-            words = zt[b][h].bitcast(F32)
+            back = bank("turned")
+            pairs = z_t[b][h].bitcast(F32)
             for g in range(2):
                 for u in range(2):
                     nc.tensor.transpose(
-                        back[:, 256 * g + 128 * u : 256 * g + 128 * u + 128],
-                        words[:, g, u:256:2],
-                        ident[:],
+                        back[:, P * (2 * g + u) : P * (2 * g + u + 1)], pairs[:, g, u : 2 * P : 2], ident[:]
                     )
-            lo, hi = 256 * h, 256 * h + 256
-            flat = zi[b][h][:]
+            grouped = z_grouped[b][h][:]
             nc.scalar.copy(
-                flat.bitcast(F32).rearrange("p (g m u) -> p g m u", g=2, u=2),
+                grouped.bitcast(F32).rearrange("p (g m u) -> p g m u", g=2, u=2),
                 back[:].rearrange("p (g u m) -> p g m u", g=2, u=2),
             )
-            nc.vector.quantize_mx(out=zc[b][:, lo:hi].bitcast(FP8X4), scales=zs[b][:, lo:hi], in_=flat)
+            bouts = slice(HALF * h, HALF * (h + 1))
+            nc.vector.quantize_mx(out=z_w[b][:, bouts].bitcast(FP8X4), scales=z_s[b][:, bouts], in_=grouped)
 
-        y = [held("y%d" % h, [P, 4, 256], F32) for h in range(2)]
-        yi = [held("yi%d" % h, [P, 256, 4], BF16) for h in range(2)]
-        yc = [held("yc%d" % h, [P, 256], U32) for h in range(2)]
-        ys = held("ys", [P, PAIRS], U8)
-        out0v = out_0.rearrange("(p t) m -> p t m", t=4)
-        out1v = out_1[0].rearrange("p m t -> p (m t)").bitcast(I32)
+        def order_w3():
+            nc.vector.tensor_copy(
+                w3_w[:].rearrange("p (a t c i) -> p a c t i", a=2, t=4, i=8),
+                w3_raw.bitcast(U16).rearrange("p (a c i t) -> p a c t i", a=2, t=4, i=8),
+            )
+            nc.vector.tensor_copy(
+                w3_s[:].rearrange("p (a t c i) -> p a c t i", a=2, t=4, i=16),
+                w3_s_raw[:].rearrange("p (a c i t) -> p a c t i", a=2, t=4, i=16),
+            )
 
-        ybank = {}
+        y_bank = {}
 
-        def last_product(quarter, b):
-            lo = 128 * quarter
+        def last_product(block, b):
+            bouts = slice(P * block, P * (block + 1))
             for t in range(4):
-                cols = slice(512 * b + 128 * t, 512 * b + 128 * t + 128)
+                cols = slice(N * b + P * t, N * b + P * (t + 1))
                 nc.tensor.matmul_mx(
-                    out=ybank[quarter][:, 128 * t : 128 * t + 128],
-                    lhsT=w3c[:, cols].bitcast(FP4X4),
-                    lhsT_scale=late["w3s"][:, cols],
-                    rhs=zc[b][:, lo : lo + 128].bitcast(FP8X4),
-                    rhs_scale=zs[b][:, lo : lo + 128],
+                    out=y_bank[block][:, P * t : P * (t + 1)],
+                    lhsT=w3_w[:, cols].bitcast(FP4X4),
+                    lhsT_scale=w3_s[:, cols],
+                    rhs=z_w[b][:, bouts].bitcast(FP8X4),
+                    rhs_scale=z_s[b][:, bouts],
                     start=(b == 0 and t == 0),
                     stop=(b == 1 and t == 3),
                 )
 
-        def finish(h):
-            og_t = late["og"]
-            for u in range(2):
-                acc = ybank[2 * h + u]
-                last_product(2 * h + u, 1)
-                if u == 0:
-                    for t in range(4):
-                        nc.scalar.activation(
-                            y[h][:, t, 0:128], acc[:, 128 * t : 128 * t + 128], ACT.Copy,
-                            scale=og_t[:, t : t + 1],
-                        )
-                else:
-                    nc.vector.tensor_tensor(
-                        y[h][:, :, 128:256],
-                        acc[:].rearrange("p (t m) -> p t m", t=4),
-                        og_t[:].unsqueeze(2).to_broadcast([P, 4, 128]),
-                        ALU.mult,
-                    )
-            nc.sync.dma_start(out0v[:, :, 256 * h : 256 * h + 256], y[h][:])
-            nc.vector.tensor_copy(
-                yi[h][:].rearrange("p (c i) t -> p c t i", i=4),
-                y[h][:].rearrange("p t (c i) -> p c t i", i=4),
+        y = [held("y%d" % h, [P, 4, HALF], F32) for h in range(2)]
+        y_grouped = [held("y_grouped%d" % h, [P, HALF, 4], BF16) for h in range(2)]
+        y_w = [held("y_w%d" % h, [P, HALF], U32) for h in range(2)]
+        y_s = held("y_s", [P, PAIRS], U8)
+        out_0_view = out_0.rearrange("(p t) m -> p t m", t=4)
+        out_1_view = out_1[0].rearrange("p m t -> p (m t)").bitcast(I32)
+
+        def finish(h, ogain_t):
+            bouts = slice(HALF * h, HALF * (h + 1))
+
+            def grouped_and_plain(u):
+                cols = slice(P * u, P * (u + 1))
+                return (
+                    y_grouped[h][:, cols, :].rearrange("p (c i) t -> p c t i", i=4),
+                    y[h][:, :, cols].rearrange("p t (c i) -> p c t i", i=4),
+                )
+
+            last_product(2 * h, 1)
+            for t in range(4):
+                nc.scalar.activation(
+                    y[h][:, t, 0:P], y_bank[2 * h][:, P * t : P * (t + 1)], ACT.Copy,
+                    scale=ogain_t[:, t : t + 1],
+                )
+            nc.scalar.copy(*grouped_and_plain(0))
+            last_product(2 * h + 1, 1)
+            nc.vector.tensor_tensor(
+                y[h][:, :, P:HALF],
+                y_bank[2 * h + 1][:].rearrange("p (t m) -> p t m", t=4),
+                ogain_t[:].unsqueeze(2).to_broadcast([P, 4, P]),
+                ALU.mult,
             )
+            nc.sync.dma_start(out_0_view[:, :, bouts], y[h][:])
+            nc.vector.tensor_copy(*grouped_and_plain(1))
             nc.vector.quantize_mx(
-                out=yc[h][:].bitcast(FP8X4),
-                scales=ys[:, 256 * h : 256 * h + 256],
-                in_=yi[h][:].rearrange("p m t -> p (m t)"),
+                out=y_w[h][:].bitcast(FP8X4),
+                scales=y_s[:, bouts],
+                in_=y_grouped[h][:].rearrange("p m t -> p (m t)"),
             )
-            nc.sync.dma_start(out1v[:, 256 * h : 256 * h + 256], yc[h][:].bitcast(I32))
+            nc.sync.dma_start(out_1_view[:, bouts], y_w[h][:].bitcast(I32))
 
-        def deal_w3():
-            w3s = late["w3s"] = held("w3s", [P, 2 * N], U8)
-            w3raw = held("w3raw", [P, 2 * N], U16, "stage2")
-            nc.scalar.dma_start(
-                w3raw[:].bitcast(I32).rearrange("p (a c) -> p a c", a=2),
-                w3_words.rearrange("a p c -> p a c").bitcast(I32),
-            )
-            nc.vector.tensor_copy(
-                w3c[:].rearrange("p (a t c i) -> p a c t i", a=2, t=4, i=8),
-                w3raw[:].rearrange("p (a c i t) -> p a c t i", a=2, t=4, i=8),
-            )
-            nc.vector.tensor_copy(
-                w3s[:].rearrange("p (a t c i) -> p a c t i", a=2, t=4, i=16),
-                w3s_raw[:].rearrange("p (a c i t) -> p a c t i", a=2, t=4, i=16),
-            )
-            late["og"] = held("og_t", [P, 4], F32, "stage3")
-            nc.sync.dma_start(late["og"][:], ogain.rearrange("(p t) -> p t", t=4))
+        for s in range(CTR_LEAD - 2):
+            pick_ctr(s)
+        order_w3()
+        ogain_t = held("ogain_t", [P, 4], F32, "w3_scales_then_ogain")
+        nc.sync.dma_start(ogain_t[:], ogain.rearrange("(p t) -> p t", t=4))
+        for a in range(2):
+            quantize_w1(0, a)
+            w1_raw[1, a] = held("w1_raw1%d" % a, [P, w1_cols], F32, "w1_next%d" % a)[:]
+            load_w1(1, a)
+            pick_ctr(CTR_LEAD - 2 + a)
 
-        for s in range(3):
-            make_ctr(s)
-        deal_w3()
-        round_w1(0, 0, False)
-        make_ctr(3)
-        round_w1(0, 1, False)
-        make_ctr(4)
-        for s in range(8):
+        for s in range(SLICES):
             make_att(s)
-            if s < 7:
+            if s < SLICES - 1:
                 pick_att(s, 0, PAIRS)
             if s > 0:
-                make_z(s - 1, 0, 4)
-            if s == 1:
-                load_w1(1)
-            if s in (2, 3):
-                round_w1(1, s - 2, False)
-            if s + 5 < 8:
-                make_ctr(s + 5)
+                make_z(s - 1, 0, PAIRS)
+            if s + CTR_LEAD < SLICES:
+                pick_ctr(s + CTR_LEAD)
+            if s in (1, 2):
+                quantize_w1(1, s - 1)
             if s in (4, 5):
                 quantize_z(0, s - 4)
-        pick_att(7, 0, 256)
-        make_z(7, 0, 2)
-        pick_att(7, 256, 512)
-        make_z(7, 2, 4)
+
+        for h in range(2):
+            pick_att(SLICES - 1, HALF * h, HALF * (h + 1))
+            make_z(SLICES - 1, HALF * h, HALF * (h + 1))
         for h in range(2):
             quantize_z(1, h)
-        ybank[2] = bank_for("acc", 3)
-        ybank[3] = bank_for("acc", 3)
-        ybank[0] = bank_for("second", 1)
-        ybank[1] = bank_for("first", 2)
-        for quarter in (2, 3, 0, 1):
-            last_product(quarter, 0)
+        for block, role in ((2, "product"), (3, "product"), (0, "second"), (1, "first")):
+            y_bank[block] = bank(role)
+        for block in y_bank:
+            last_product(block, 0)
         for h in range(2):
-            finish(h)
+            finish(h, ogain_t)
         for q in range(4):
             queue = nc.sync if q % 2 == 0 else nc.scalar
             queue.dma_start(
-                out_2[0, 4 * q : 4 * q + 4, :].bitcast(I32), ys[32 * q : 32 * q + 4, :].bitcast(I32)
+                out_2[0, 4 * q : 4 * q + 4, :].bitcast(I32), y_s[32 * q : 32 * q + 4, :].bitcast(I32)
             )

from contextlib import ExitStack

import concourse.mybir as mybir
from concourse.masks import make_identity

K, T, S, H, PAIRS, N = 1024, 4096, 1024, 1024, 512, 512
FLOPS = 2 * (2 * K * H * S + H * N * PAIRS)

F32 = mybir.dt.float32
BF16 = mybir.dt.bfloat16
I32 = mybir.dt.int32
U32 = mybir.dt.uint32
U16 = mybir.dt.uint16
U8 = mybir.dt.uint8
FP8X4 = mybir.dt.float8_e4m3fn_x4
FP4X4 = mybir.dt.float4_e2m1fn_x4
ACT = mybir.ActivationFunctionType
ALU = mybir.AluOpType

P = 128
BANK = 512
SLICES = H // P
HALF = PAIRS // 2
CTR_LEAD = 5
SCALE_ROW0 = 96
VEC_ROW0 = 112


def tile_list_bout_corner_planner_kernel(
    tc, tab_words, tab_scales, offs, pos1, pos2, w1, w2_words, w2_scales, bc, cgain,
    w3_words, w3_scales, ogain, out_0, out_1, out_2,
):
    nc = tc.nc
    with ExitStack() as ctx:
        keep = ctx.enter_context(tc.tile_pool(name="keep", bufs=1))
        ring = ctx.enter_context(tc.tile_pool(name="ring", bufs=2))
        psum = ctx.enter_context(tc.psum_pool(name="psum", bufs=1))

        def held(name, shape, dtype, tag=None):
            return keep.tile(shape, dtype, name=name, tag=tag or name, align_bytes=64)

        turns = {}

        def in_turn(name, count):
            turns[name] = turns.get(name, -1) + 1
            return "%s%d" % (name, turns[name] % count)

        bank_counts = {"product": 3, "first": 2, "second": 1, "turned": 2}

        def bank(role):
            return psum.tile([P, BANK], F32, name=in_turn(role, bank_counts[role]))

        offs_t = held("offs_t", [P, S // 16], U16)
        pos1_t = held("pos1_t", [P, PAIRS // 16], U16)
        pos2_t = held("pos2_t", [P, PAIRS // 16], U16)
        tab_w = [held("tab_w%d" % a, [P, T], U16, "table%d" % a) for a in range(2)]
        tab_s = held("tab_s", [P, T], U8)
        v_w = [held("v_w%d" % a, [P, S], U16) for a in range(2)]
        v_s_rows = held("v_s_rows", [P, S], U8, "late_weights")
        v_s = [held("v_s%d" % a, [P, S], U8) for a in range(2)]
        w2_first = held("w2_first", [P, 2, BANK], I32)
        w2_s = held("w2_s", [P, 2 * H], U8)
        w3_s_raw = held("w3_s_raw", [P, 2 * N], U8, "w3_scales_then_ogain")
        w3_w = held("w3_w", [P, 2 * N], U16)
        w3_s = held("w3_s", [P, 2 * N], U8)
        w1_w = [[held("w1_w%d%d" % (b, a), [P, BANK], U32) for a in range(2)] for b in range(2)]
        w1_s = [[held("w1_s%d%d" % (b, a), [P, BANK], U8) for a in range(2)] for b in range(2)]
        ident = held("ident", [P, P], F32)
        vec_rows = held("vec_rows", [P, P], F32)
        vec = held("vec", [P, 2 * SLICES], F32)
        gain = held("gain", [P, SLICES, PAIRS], F32)

        nc.vector.memset(w2_s[:].bitcast(I32), 0)
        nc.vector.memset(vec_rows[0:64, :], 0.0)
        nc.vector.memset(vec_rows[64:VEC_ROW0, :], 0.0)
        nc.vector.memset(tab_s[0:64, :].bitcast(I32), 0)
        nc.vector.memset(tab_s[64:SCALE_ROW0, :].bitcast(I32), 0)
        make_identity(nc, ident[:])
        for a in range(2):
            nc.vector.memset(v_s[a][:].bitcast(I32), 0)

        w2_view = w2_words.rearrange("a p c i -> p a (c i)").bitcast(I32)
        w1_view = w1.rearrange("(a p j) c -> a p j c", a=2, j=4)
        nc.sync.dma_start(offs_t[:], offs)
        nc.sync.dma_start(
            tab_s[SCALE_ROW0:P, :].bitcast(I32), tab_scales.rearrange("a q t -> (a q) t").bitcast(I32)
        )
        nc.sync.dma_start(vec_rows[VEC_ROW0 : VEC_ROW0 + SLICES, :], bc.rearrange("(s p) -> s p", p=P))
        nc.sync.dma_start(vec_rows[VEC_ROW0 + SLICES : P, :], cgain.rearrange("(s p) -> s p", p=P))
        nc.sync.dma_start(tab_w[0][:].bitcast(I32), tab_words[0].bitcast(I32))
        nc.sync.dma_start(pos1_t[:], pos1)
        nc.sync.dma_start(pos2_t[:], pos2)
        nc.sync.dma_start(tab_w[1][:].bitcast(I32), tab_words[1].bitcast(I32))
        nc.sync.dma_start(w2_first[:], w2_view[:, :, 0:BANK])

        def load_scale_rows(tile, scales):
            for q in range(4):
                nc.gpsimd.dma_start(
                    tile[32 * q : 32 * q + 4, :].bitcast(I32).rearrange("p (a c) -> p a c", a=2),
                    scales[:, 4 * q : 4 * q + 4, :].rearrange("a r c -> r a c").bitcast(I32),
                )

        load_scale_rows(w2_s, w2_scales)

        vec_bank = bank("turned")
        nc.tensor.transpose(vec_bank[:, 0:P], vec_rows[:], ident[:])
        nc.scalar.copy(vec[:], vec_bank[:, VEC_ROW0:P])
        nc.gpsimd.memset(w3_s_raw[:].bitcast(I32), 0)
        load_scale_rows(w3_s_raw, w3_scales)

        nc.vector.tensor_copy(v_s_rows[:], tab_s[:].indirect(offs_t[:]))
        for a in range(2):
            for q in range(4):
                row = SCALE_ROW0 + 16 * a + 4 * q
                nc.sync.dma_start(
                    v_s[a][32 * q : 32 * q + 4, :].bitcast(I32), v_s_rows[row : row + 4, :].bitcast(I32)
                )
        nc.vector.tensor_copy(v_w[0][:], tab_w[0][:].indirect(offs_t[:]))
        for h in range(2):
            nc.vector.tensor_copy(
                v_w[1][:, BANK * h : BANK * (h + 1)], tab_w[1][:].indirect(offs_t[:, 32 * h : 32 * (h + 1)])
            )

        w1_cols = 4 * BANK
        w1_first = held("w1_first", [P, 2 * w1_cols], F32, "late_weights")
        w1_raw = {(0, a): w1_first[:, w1_cols * a : w1_cols * (a + 1)] for a in range(2)}
        packed_in = held("packed_in", [P, 2 * BANK + N], I32, "table1")
        w2_second = packed_in[:, 0 : 2 * BANK]
        w3_raw = packed_in[:, 2 * BANK : 2 * BANK + N]
        w2_w = [w2_first[:], w2_second.rearrange("p (a c) -> p a c", a=2)]

        def w1_rows(b, a):
            return w1_raw[b, a].rearrange("p (j c) -> p j c", j=4)

        def load_w1(b, a):
            nc.sync.dma_start(w1_rows(b, a), w1_view[a, :, :, BANK * b : BANK * (b + 1)])

        nc.sync.dma_start(
            w3_raw.rearrange("p (a c) -> p a c", a=2), w3_words.rearrange("a p c -> p a c").bitcast(I32)
        )
        load_w1(0, 0)
        nc.sync.dma_start(w2_w[1], w2_view[:, :, BANK : 2 * BANK])
        load_w1(0, 1)

        def quantize_w1(b, a):
            grouped = held("w1_grouped%d%d" % (b, a), [P, BANK, 4], BF16, "w1_next%d" % a if b == 0 else None)
            nc.scalar.copy(
                grouped[:].rearrange("p (c i) j -> p c j i", i=4),
                w1_rows(b, a).rearrange("p j (c i) -> p c j i", i=4),
            )
            nc.vector.quantize_mx(
                out=w1_w[b][a][:].bitcast(FP8X4),
                scales=w1_s[b][a][:],
                in_=grouped[:].rearrange("p c j -> p (c j)"),
            )

        def first_product(words, scales, h):
            acc = bank("product")
            cols = slice(BANK * h, BANK * (h + 1))
            for a in range(2):
                nc.tensor.matmul_mx(
                    out=acc[:],
                    lhsT=words[a].bitcast(FP8X4),
                    lhsT_scale=scales[a],
                    rhs=v_w[a][:, cols].bitcast(FP4X4),
                    rhs_scale=v_s[a][:, cols],
                    start=(a == 0),
                    stop=(a == 1),
                )
            return acc

        att, att1, att2, ctr1, ctr2 = {}, {}, {}, {}, {}

        def pick_ctr(s):
            b, t = divmod(s, 4)
            bounded = ring.tile([P, S], F32, name="bounded", bufs=4)
            nc.scalar.copy(gain[:, s, :], vec[:, SLICES + s : SLICES + s + 1].to_broadcast([P, PAIRS]))
            for h in range(2):
                acc = first_product(
                    [w2_w[b][:, a, P * t : P * (t + 1)] for a in range(2)],
                    [w2_s[:, H * a + P * s : H * a + P * (s + 1)] for a in range(2)],
                    h,
                )
                nc.scalar.activation(
                    bounded[:, BANK * h : BANK * (h + 1)], acc[:], ACT.Tanh, bias=vec[:, s : s + 1]
                )
            ctr1[s] = ring.tile([P, PAIRS], F32, name="ctr1", bufs=SLICES)
            ctr2[s] = ring.tile([P, PAIRS], F32, name="ctr2", bufs=SLICES)
            nc.vector.tensor_tensor(ctr2[s][:], bounded[:].indirect(pos2_t[:]), gain[:, s, :], ALU.mult)
            nc.vector.tensor_tensor(ctr1[s][:], bounded[:].indirect(pos1_t[:]), gain[:, s, :], ALU.mult)

        def make_att(s):
            b, t = divmod(s, 4)
            att[s] = ring.tile([P, S], F32, name="att", bufs=4)
            for h in range(2):
                acc = first_product(
                    [w1_w[b][a][:, P * t : P * (t + 1)] for a in range(2)],
                    [w1_s[b][a][:, P * t : P * (t + 1)] for a in range(2)],
                    h,
                )
                nc.scalar.copy(att[s][:, BANK * h : BANK * (h + 1)], acc[:])

        def pick_att(s, lo, hi):
            if lo == 0:
                att1[s] = ring.tile([P, hi], F32, name="att1", bufs=3)[:]
                att2[s] = ring.tile([P, hi], F32, name="att2", bufs=3)[:]
            else:
                both = held(in_turn("second_sb", 2), [P, BANK], F32)
                att1[s], att2[s] = both[:, 0:HALF], both[:, HALF:BANK]
            entries = slice(lo // 16, hi // 16)
            nc.vector.tensor_copy(att2[s], att[s][:].indirect(pos2_t[:, entries]))
            nc.vector.tensor_copy(att1[s], att[s][:].indirect(pos1_t[:, entries]))

        z_t0 = held("z_t0", [P, 4, BANK], BF16)
        z_t = [
            [z_t0[:, 0:2, :], z_t0[:, 2:4, :]],
            [held("z_t1%d" % h, [P, 2, BANK], BF16)[:] for h in range(2)],
        ]
        z_grouped = [[held("z_grouped%d%d" % (b, h), [P, 4 * HALF], BF16) for h in range(2)] for b in range(2)]
        z_w = [held("z_w%d" % b, [P, PAIRS], U32) for b in range(2)]
        z_s = [held("z_s%d" % b, [P, PAIRS], U8) for b in range(2)]

        def make_z(s, lo, hi):
            b, t = divmod(s, 4)
            first = bank("first")
            second = bank("second" if lo == 0 else "product")
            width = hi - lo
            blocks = range(width // P)
            for acc, picked_ctr, picked_att in ((second, ctr1[s], att2[s]), (first, ctr2[s], att1[s])):
                for g in blocks:
                    nc.tensor.matmul(
                        acc[:, P * g : P * (g + 1)], picked_ctr[:, lo + P * g : lo + P * (g + 1)],
                        ident[:], start=(g == 0), stop=False, is_transpose=True,
                    )
                for g in blocks:
                    nc.tensor.matmul(
                        acc[:, P * g : P * (g + 1)], picked_att[:, P * g : P * (g + 1)],
                        ident[:], start=False, stop=(g == blocks[-1]), is_transpose=True,
                    )
            second_sb = held(in_turn("second_sb", 2), [P, BANK], F32)
            nc.scalar.copy(second_sb[:, 0:width], second[:, 0:width])
            if b == 0:
                parts = [(z_t0[:], slice(0, width))]
            else:
                parts = [
                    (z_t[1][h], slice(HALF * h - lo, HALF * (h + 1) - lo))
                    for h in range(lo // HALF, hi // HALF)
                ]
            for dst, cols in parts:
                nc.vector.tensor_tensor(
                    dst[:, :, P * t : P * (t + 1)],
                    first[:, cols].rearrange("p (g r) -> p g r", r=P),
                    second_sb[:, cols].rearrange("p (g r) -> p g r", r=P),
                    ALU.max,
                )

        def quantize_z(b, h):
            back = bank("turned")
            pairs = z_t[b][h].bitcast(F32)
            for g in range(2):
                for u in range(2):
                    nc.tensor.transpose(
                        back[:, P * (2 * g + u) : P * (2 * g + u + 1)], pairs[:, g, u : 2 * P : 2], ident[:]
                    )
            grouped = z_grouped[b][h][:]
            nc.scalar.copy(
                grouped.bitcast(F32).rearrange("p (g m u) -> p g m u", g=2, u=2),
                back[:].rearrange("p (g u m) -> p g m u", g=2, u=2),
            )
            bouts = slice(HALF * h, HALF * (h + 1))
            nc.vector.quantize_mx(out=z_w[b][:, bouts].bitcast(FP8X4), scales=z_s[b][:, bouts], in_=grouped)

        def order_w3():
            nc.vector.tensor_copy(
                w3_w[:].rearrange("p (a t c i) -> p a c t i", a=2, t=4, i=8),
                w3_raw.bitcast(U16).rearrange("p (a c i t) -> p a c t i", a=2, t=4, i=8),
            )
            nc.vector.tensor_copy(
                w3_s[:].rearrange("p (a t c i) -> p a c t i", a=2, t=4, i=16),
                w3_s_raw[:].rearrange("p (a c i t) -> p a c t i", a=2, t=4, i=16),
            )

        y_bank = {}

        def last_product(block, b):
            bouts = slice(P * block, P * (block + 1))
            for t in range(4):
                cols = slice(N * b + P * t, N * b + P * (t + 1))
                nc.tensor.matmul_mx(
                    out=y_bank[block][:, P * t : P * (t + 1)],
                    lhsT=w3_w[:, cols].bitcast(FP4X4),
                    lhsT_scale=w3_s[:, cols],
                    rhs=z_w[b][:, bouts].bitcast(FP8X4),
                    rhs_scale=z_s[b][:, bouts],
                    start=(b == 0 and t == 0),
                    stop=(b == 1 and t == 3),
                )

        y = [held("y%d" % h, [P, 4, HALF], F32) for h in range(2)]
        y_grouped = [held("y_grouped%d" % h, [P, HALF, 4], BF16) for h in range(2)]
        y_w = [held("y_w%d" % h, [P, HALF], U32) for h in range(2)]
        y_s = held("y_s", [P, PAIRS], U8)
        out_0_view = out_0.rearrange("(p t) m -> p t m", t=4)
        out_1_view = out_1[0].rearrange("p m t -> p (m t)").bitcast(I32)

        def finish(h, ogain_t):
            bouts = slice(HALF * h, HALF * (h + 1))

            def grouped_and_plain(u):
                cols = slice(P * u, P * (u + 1))
                return (
                    y_grouped[h][:, cols, :].rearrange("p (c i) t -> p c t i", i=4),
                    y[h][:, :, cols].rearrange("p t (c i) -> p c t i", i=4),
                )

            last_product(2 * h, 1)
            for t in range(4):
                nc.scalar.activation(
                    y[h][:, t, 0:P], y_bank[2 * h][:, P * t : P * (t + 1)], ACT.Copy,
                    scale=ogain_t[:, t : t + 1],
                )
            nc.scalar.copy(*grouped_and_plain(0))
            last_product(2 * h + 1, 1)
            nc.vector.tensor_tensor(
                y[h][:, :, P:HALF],
                y_bank[2 * h + 1][:].rearrange("p (t m) -> p t m", t=4),
                ogain_t[:].unsqueeze(2).to_broadcast([P, 4, P]),
                ALU.mult,
            )
            nc.sync.dma_start(out_0_view[:, :, bouts], y[h][:])
            nc.vector.tensor_copy(*grouped_and_plain(1))
            nc.vector.quantize_mx(
                out=y_w[h][:].bitcast(FP8X4),
                scales=y_s[:, bouts],
                in_=y_grouped[h][:].rearrange("p m t -> p (m t)"),
            )
            nc.sync.dma_start(out_1_view[:, bouts], y_w[h][:].bitcast(I32))

        for s in range(CTR_LEAD - 2):
            pick_ctr(s)
        order_w3()
        ogain_t = held("ogain_t", [P, 4], F32, "w3_scales_then_ogain")
        nc.sync.dma_start(ogain_t[:], ogain.rearrange("(p t) -> p t", t=4))
        for a in range(2):
            quantize_w1(0, a)
            w1_raw[1, a] = held("w1_raw1%d" % a, [P, w1_cols], F32, "w1_next%d" % a)[:]
            load_w1(1, a)
            pick_ctr(CTR_LEAD - 2 + a)

        for s in range(SLICES):
            make_att(s)
            if s < SLICES - 1:
                pick_att(s, 0, PAIRS)
            if s > 0:
                make_z(s - 1, 0, PAIRS)
            if s + CTR_LEAD < SLICES:
                pick_ctr(s + CTR_LEAD)
            if s in (1, 2):
                quantize_w1(1, s - 1)
            if s in (4, 5):
                quantize_z(0, s - 4)

        for h in range(2):
            pick_att(SLICES - 1, HALF * h, HALF * (h + 1))
            make_z(SLICES - 1, HALF * h, HALF * (h + 1))
        for h in range(2):
            quantize_z(1, h)
        for block, role in ((2, "product"), (3, "product"), (0, "second"), (1, "first")):
            y_bank[block] = bank(role)
        for block in y_bank:
            last_product(block, 0)
        for h in range(2):
            finish(h, ogain_t)
        for q in range(4):
            queue = nc.sync if q % 2 == 0 else nc.scalar
            queue.dma_start(
                out_2[0, 4 * q : 4 * q + 4, :].bitcast(I32), y_s[32 * q : 32 * q + 4, :].bitcast(I32)
            )
